import numpy as np
import ml_dtypes


def mxq(x, axis, fmt="e4m3"):
    dtype, down = {"e4m3": (ml_dtypes.float8_e4m3fn, 7), "e5m2": (ml_dtypes.float8_e5m2, 14)}[fmt]
    v = np.moveaxis(np.asarray(x, np.float32).astype(ml_dtypes.bfloat16).astype(np.float64), axis, -1)
    blocks = v.reshape(v.shape[:-1] + (-1, 32))
    amax = np.abs(blocks).max(-1, keepdims=True)
    byte = np.maximum(np.where(amax > 0, np.frexp(amax)[1] - 1 + 127, 0) - down, 1)
    scale = np.exp2(byte - 127.0)
    codes = (blocks / scale).astype(np.float32).astype(dtype).astype(np.float64)
    return np.moveaxis((codes * scale).reshape(v.shape), -1, axis)


WIDE = False


def mx_kscale(k):
    if not WIDE:
        return np.ones(k)
    levels = np.array([10, -10, 5, -5, 0])
    if k % 512:
        return np.exp2(np.random.permutation(np.resize(levels, k // 32))).repeat(32)
    a = np.empty((k // 512, 16))
    for p in range(k // 512):
        a[p, :8] = np.random.permutation(np.resize(levels, 8))
        for g in range(8):
            far = levels[np.abs(levels - a[p, g]) >= 10]
            a[p, g + 8] = far[np.random.randint(len(far))]
    return np.exp2(a.ravel()).repeat(32)


def f64(x):
    return np.asarray(x).astype(np.float64)


def striped(idx):
    return np.tile(idx.reshape(-1, 16).T, (8, 1)).astype(np.uint16)


def unstriped(offs):
    return offs[:16].T.reshape(-1).astype(np.int64)


def pack_weight(w):
    k, n = w.shape
    w = f64(np.asarray(w, np.float32).astype(ml_dtypes.bfloat16)).reshape(k // 32, 32, n)
    amax = np.abs(w).max(1)
    byte = np.clip(np.where(amax > 0, np.frexp(amax)[1] - 1 + 127 - 7, 1), 1, 254)
    scaled = (w * np.exp2(127.0 - byte)[:, None, :]).reshape(k, n).astype(np.float32)
    words = np.ascontiguousarray(scaled.reshape(k // 512, 128, 4, n).transpose(0, 1, 3, 2)).astype(ml_dtypes.float8_e4m3fn).view(np.uint8)
    return words, np.ascontiguousarray(byte.astype(np.uint8).reshape(k // 512, 16, n))


def unpack_weight(words, scales):
    g, p, n, _ = words.shape
    vals = np.ascontiguousarray(words).view(ml_dtypes.float8_e4m3fn).astype(np.float64) * np.repeat(np.exp2(scales.astype(np.float64) - 127.0), 8, axis=1)[..., None]
    return vals.transpose(0, 1, 3, 2).reshape(g * 512, n)


def sigmoid(v):
    return 1.0 / (1.0 + np.exp(-np.maximum(v, -700.0)))


K, T, S, N, U = 1024, 2048, 512, 128, 1024


def setup_inputs():
    n = np.random.standard_normal
    s = mx_kscale(K)[:, None]
    packed_xT = pack_weight(n((K, T)) * s)
    return {
        "x_words": packed_xT[0],
        "x_scales": packed_xT[1],
        "mem": n((N, U)).astype(np.float32),
        "w1": (n((K, N)) / np.sqrt(K) / s).astype(np.float32),
        "w2": (n((K, N)) / np.sqrt(K) / s).astype(np.float32),
        "offs": striped(np.random.permutation(T)[:S]),
        "slot": striped(np.random.permutation(U)[:S]),
    }


def reference(x_words, x_scales, mem, w1, w2, offs, slot):
    old = f64(mem)[:, unstriped(slot)]
    xq = unpack_weight(x_words, x_scales)[:, unstriped(offs)]
    g = sigmoid(mxq(f64(w2), 0, "e4m3").T @ xq)
    y = np.tanh(mxq(f64(w1), 0, "e4m3").T @ xq)
    out = f64(mem).copy()
    out[:, unstriped(slot)] = old + g * (y - old)
    return out

@@ -1,0 +1,130 @@
+from contextlib import ExitStack
+
+import concourse.mybir as mybir
+
+K, T, S, N, U = 1024, 2048, 512, 128, 1024
+FLOPS = 2 * 2 * K * N * S
+
+F32 = mybir.dt.float32
+BF16 = mybir.dt.bfloat16
+I32 = mybir.dt.int32
+U32 = mybir.dt.uint32
+U16 = mybir.dt.uint16
+U8 = mybir.dt.uint8
+FP8X4 = mybir.dt.float8_e4m3fn_x4
+ACT = mybir.ActivationFunctionType
+ALU = mybir.AluOpType
+
+P = 128
+PACK = 4
+PASSES = K // (P * PACK)
+HALF = S // 2
+LANES = 16
+
+
+def tile_picked_gmem_tanh_p_kernel(tc, x_words, x_scales, mem, w1, w2, offs, slot, out):
+    nc = tc.nc
+    with ExitStack() as ctx:
+        sb = ctx.enter_context(tc.tile_pool(name="sb", bufs=1))
+        ps = ctx.enter_context(tc.psum_pool(name="ps", bufs=1))
+
+        offs_t = sb.tile([P, S // LANES], U16, name="offs_t")
+        slot_t = sb.tile([P, S // LANES], U16, name="slot_t")
+        planes = sb.tile([P, T], U8, name="planes", align_bytes=64)
+        nc.vector.memset(planes[:].bitcast(I32), 0)
+        warm_in = sb.tile([P, 1], F32, name="warm_in")
+        warm_out = sb.tile([P, 1], F32, name="warm_out")
+        nc.vector.memset(warm_in[:], 0.0)
+
+        raw1 = sb.tile([P, PASSES, PACK, N], F32, name="raw1")
+        raw2 = [sb.tile([P, PACK, N], F32, name="raw2_%d" % g) for g in range(PASSES)]
+        table = [sb.tile([P, T], U32, name="table%d" % g, align_bytes=64) for g in range(PASSES)]
+        window = sb.tile([P, U], F32, name="window", align_bytes=64)
+        w2_rows = w2.rearrange("(g p j) n -> g p j n", g=PASSES, j=PACK)
+
+        nc.sync.dma_start(offs_t[:], offs)
+        nc.sync.dma_start(raw1[:], w1.rearrange("(g p j) n -> p g j n", g=PASSES, j=PACK))
+        for q in range(4):
+            nc.sync.dma_start(
+                planes[32 * q : 32 * q + 4 * PASSES, :].bitcast(I32),
+                x_scales[:, 4 * q : 4 * q + 4, :].bitcast(I32),
+            )
+        nc.sync.dma_start(raw2[0][:], w2_rows[0])
+        for g in range(PASSES):
+            nc.sync.dma_start(table[g][:].bitcast(I32), x_words[g].rearrange("p n t -> p (n t)").bitcast(I32))
+        nc.sync.dma_start(raw2[1][:], w2_rows[1])
+        nc.sync.dma_start(slot_t[:], slot)
+        nc.sync.dma_start(window[:], mem)
+        nc.scalar.activation(warm_out[:], warm_in[:], ACT.Sigmoid)
+
+        grouped1 = sb.tile([P, PASSES, N, PACK], BF16, name="grouped1", align_bytes=64)
+        nc.vector.tensor_copy(grouped1[:], raw1[:].rearrange("p g j n -> p g n j"))
+        codes1 = sb.tile([P, PASSES * N], U32, name="codes1", align_bytes=64)
+        scales1 = sb.tile([P, PASSES * N], U8, name="scales1", align_bytes=64)
+        nc.vector.quantize_mx(
+            out=codes1[:].bitcast(FP8X4), scales=scales1[:], in_=grouped1[:].rearrange("p g n j -> p (g n j)")
+        )
+        codes = [[codes1[:, g * N : (g + 1) * N] for g in range(PASSES)], []]
+        scales = [[scales1[:, g * N : (g + 1) * N] for g in range(PASSES)], []]
+
+        def quantise_gate(g):
+            grouped = sb.tile([P, N, PACK], BF16, name="grouped2_%d" % g, align_bytes=64)
+            nc.scalar.copy(grouped[:], raw2[g][:].rearrange("p j n -> p n j"))
+            c = sb.tile([P, N], U32, name="codes2_%d" % g, align_bytes=64)
+            s = sb.tile([P, N], U8, name="scales2_%d" % g, align_bytes=64)
+            nc.vector.quantize_mx(
+                out=c[:].bitcast(FP8X4), scales=s[:], in_=grouped[:].rearrange("p n j -> p (n j)")
+            )
+            codes[1].append(c[:])
+            scales[1].append(s[:])
+
+        quantise_gate(0)
+        x_planes = sb.tile([P, S], U8, name="x_planes", align_bytes=64)
+        nc.vector.tensor_copy(x_planes[:], planes[:].indirect(offs_t[:]))
+        first = sb.tile([P, S], U32, name="first", align_bytes=64)
+        nc.vector.tensor_copy(first[:], table[0][:].indirect(offs_t[:]))
+
+        acc = [[ps.tile([P, 512], F32, name="acc%d_%d" % (h, i)) for i in range(2)] for h in range(2)]
+
+        def product(h, i, g, words):
+            nc.tensor.matmul_mx(
+                out=acc[h][i][:, :HALF],
+                lhsT=codes[i][g].bitcast(FP8X4),
+                lhsT_scale=scales[i][g],
+                rhs=words.bitcast(FP8X4),
+                rhs_scale=x_planes[4 * g :, h * HALF : (h + 1) * HALF],
+                start=(g == 0),
+                stop=(g == PASSES - 1),
+            )
+
+        for h in range(2):
+            for i in range(2):
+                product(h, i, 0, first[:, h * HALF : (h + 1) * HALF])
+
+        cand = sb.tile([P, S], F32, name="cand", align_bytes=64)
+        keep = sb.tile([P, S], F32, name="keep", align_bytes=64)
+        diff = sb.tile([P, S], F32, name="diff", align_bytes=64)
+        rest = sb.tile([P, S], F32, name="rest", align_bytes=64)
+        cols = [slice(h * HALF, (h + 1) * HALF) for h in range(2)]
+        lcols = [slice(h * HALF // LANES, (h + 1) * HALF // LANES) for h in range(2)]
+        second = [sb.tile([P, HALF], U32, name="second%d" % h, align_bytes=64) for h in range(2)]
+        for h in range(2):
+            nc.vector.tensor_copy(second[h][:], table[1][:].indirect(offs_t[:, lcols[h]]))
+            product(h, 0, 1, second[h][:])
+        quantise_gate(1)
+        for h in range(2):
+            nc.scalar.activation(cand[:, cols[h]], acc[h][0][:, :HALF], ACT.Tanh)
+        for h in range(2):
+            product(h, 1, 1, second[h][:])
+            nc.scalar.activation(keep[:, cols[h]], acc[h][1][:, :HALF], ACT.Sigmoid, scale=-1.0)
+        for h in range(2):
+            nc.vector.tensor_tensor(
+                diff[:, cols[h]], window[:].indirect(slot_t[:, lcols[h]]), cand[:, cols[h]], ALU.subtract
+            )
+        for h in range(2):
+            nc.vector.tensor_tensor(rest[:, cols[h]], diff[:, cols[h]], keep[:, cols[h]], ALU.mult)
+        for h in range(2):
+            nc.vector.tensor_tensor(
+                window[:].indirect(slot_t[:, lcols[h]]), rest[:, cols[h]], cand[:, cols[h]], ALU.add
+            )
+        nc.sync.dma_start(out, window[:])

@@ -30,8 +30,9 @@ def tile_picked_gmem_tanh_p_kernel(tc, x_words, x_scales, mem, w1, w2, offs, slo
 
         offs_t = sb.tile([P, S // LANES], U16, name="offs_t")
         slot_t = sb.tile([P, S // LANES], U16, name="slot_t")
-        planes = sb.tile([P, T], U8, name="planes", align_bytes=64)
-        nc.vector.memset(planes[:].bitcast(I32), 0)
+        planes = [sb.tile([P, T], U8, name="planes%d" % g, align_bytes=64) for g in range(PASSES)]
+        for g in range(PASSES):
+            nc.vector.memset(planes[g][:].bitcast(I32), 0)
         warm_in = sb.tile([P, 1], F32, name="warm_in")
         warm_out = sb.tile([P, 1], F32, name="warm_out")
         nc.vector.memset(warm_in[:], 0.0)
@@ -42,16 +43,23 @@ def tile_picked_gmem_tanh_p_kernel(tc, x_words, x_scales, mem, w1, w2, offs, slo
         window = sb.tile([P, U], F32, name="window", align_bytes=64)
         w2_rows = w2.rearrange("(g p j) n -> g p j n", g=PASSES, j=PACK)
 
-        nc.sync.dma_start(offs_t[:], offs)
-        nc.sync.dma_start(raw1[:], w1.rearrange("(g p j) n -> p g j n", g=PASSES, j=PACK))
-        for q in range(4):
-            nc.sync.dma_start(
-                planes[32 * q : 32 * q + 4 * PASSES, :].bitcast(I32),
-                x_scales[:, 4 * q : 4 * q + 4, :].bitcast(I32),
-            )
-        nc.sync.dma_start(raw2[0][:], w2_rows[0])
-        for g in range(PASSES):
+        def load_scales(g):
+            for q in range(4):
+                nc.sync.dma_start(
+                    planes[g][32 * q + 4 * g : 32 * q + 4 * g + 4, :].bitcast(I32),
+                    x_scales[g, 4 * q : 4 * q + 4, :].bitcast(I32),
+                )
+
+        def load_words(g):
             nc.sync.dma_start(table[g][:].bitcast(I32), x_words[g].rearrange("p n t -> p (n t)").bitcast(I32))
+
+        nc.sync.dma_start(raw1[:], w1.rearrange("(g p j) n -> p g j n", g=PASSES, j=PACK))
+        nc.sync.dma_start(offs_t[:], offs)
+        load_scales(0)
+        nc.sync.dma_start(raw2[0][:], w2_rows[0])
+        load_words(0)
+        load_scales(1)
+        load_words(1)
         nc.sync.dma_start(raw2[1][:], w2_rows[1])
         nc.sync.dma_start(slot_t[:], slot)
         nc.sync.dma_start(window[:], mem)
@@ -79,10 +87,11 @@ def tile_picked_gmem_tanh_p_kernel(tc, x_words, x_scales, mem, w1, w2, offs, slo
             scales[1].append(s[:])
 
         quantise_gate(0)
-        x_planes = sb.tile([P, S], U8, name="x_planes", align_bytes=64)
-        nc.vector.tensor_copy(x_planes[:], planes[:].indirect(offs_t[:]))
+        x_planes = [sb.tile([P, S], U8, name="x_planes%d" % g, align_bytes=64) for g in range(PASSES)]
+        nc.vector.tensor_copy(x_planes[0][:], planes[0][:].indirect(offs_t[:]))
         first = sb.tile([P, S], U32, name="first", align_bytes=64)
         nc.vector.tensor_copy(first[:], table[0][:].indirect(offs_t[:]))
+        nc.vector.tensor_copy(x_planes[1][:], planes[1][:].indirect(offs_t[:]))
 
         acc = [[ps.tile([P, 512], F32, name="acc%d_%d" % (h, i)) for i in range(2)] for h in range(2)]
 
@@ -92,7 +101,7 @@ def tile_picked_gmem_tanh_p_kernel(tc, x_words, x_scales, mem, w1, w2, offs, slo
                 lhsT=codes[i][g].bitcast(FP8X4),
                 lhsT_scale=scales[i][g],
                 rhs=words.bitcast(FP8X4),
-                rhs_scale=x_planes[4 * g :, h * HALF : (h + 1) * HALF],
+                rhs_scale=x_planes[g][4 * g :, h * HALF : (h + 1) * HALF],
                 start=(g == 0),
                 stop=(g == PASSES - 1),
             )
@@ -123,8 +132,5 @@ def tile_picked_gmem_tanh_p_kernel(tc, x_words, x_scales, mem, w1, w2, offs, slo
             )
         for h in range(2):
             nc.vector.tensor_tensor(rest[:, cols[h]], diff[:, cols[h]], keep[:, cols[h]], ALU.mult)
-        for h in range(2):
-            nc.vector.tensor_tensor(
-                window[:].indirect(slot_t[:, lcols[h]]), rest[:, cols[h]], cand[:, cols[h]], ALU.add
-            )
+        nc.vector.tensor_tensor(window[:].indirect(slot_t[:]), rest[:], cand[:], ALU.add)
         nc.sync.dma_start(out, window[:])

@@ -18,8 +18,13 @@ ALU = mybir.AluOpType
 P = 128
 PACK = 4
 PASSES = K // (P * PACK)
-HALF = S // 2
-LANES = 16
+QUADRANT = 32
+SCALE_ROWS = 4
+LIST_ROWS = 16
+BANK = 512
+HALVES = 2
+HALF = S // HALVES
+CANDIDATE, GATE = 0, 1
 
 
 def tile_picked_gmem_tanh_p_kernel(tc, x_words, x_scales, mem, w1, w2, offs, slot, out):
@@ -28,109 +33,117 @@ def tile_picked_gmem_tanh_p_kernel(tc, x_words, x_scales, mem, w1, w2, offs, slo
         sb = ctx.enter_context(tc.tile_pool(name="sb", bufs=1))
         ps = ctx.enter_context(tc.psum_pool(name="ps", bufs=1))
 
-        offs_t = sb.tile([P, S // LANES], U16, name="offs_t")
-        slot_t = sb.tile([P, S // LANES], U16, name="slot_t")
-        planes = [sb.tile([P, T], U8, name="planes%d" % g, align_bytes=64) for g in range(PASSES)]
-        for g in range(PASSES):
-            nc.vector.memset(planes[g][:].bitcast(I32), 0)
-        warm_in = sb.tile([P, 1], F32, name="warm_in")
-        warm_out = sb.tile([P, 1], F32, name="warm_out")
-        nc.vector.memset(warm_in[:], 0.0)
+        offs_t = sb.tile([P, S // LIST_ROWS], U16, name="offs_t")
+        slot_t = sb.tile([P, S // LIST_ROWS], U16, name="slot_t")
 
-        raw1 = sb.tile([P, PASSES, PACK, N], F32, name="raw1")
-        raw2 = [sb.tile([P, PACK, N], F32, name="raw2_%d" % g) for g in range(PASSES)]
-        table = [sb.tile([P, T], U32, name="table%d" % g, align_bytes=64) for g in range(PASSES)]
+        scale_table = [sb.tile([P, T], U8, name="scale_table%d" % g, align_bytes=64) for g in range(PASSES)]
+        for g in range(PASSES):
+            nc.vector.memset(scale_table[g][:].bitcast(I32), 0)
+
+        w1_raw = sb.tile([P, PASSES, PACK, N], F32, name="w1_raw")
+        w2_raw = [sb.tile([P, PACK, N], F32, name="w2_raw%d" % g) for g in range(PASSES)]
+        word_table = [sb.tile([P, T], U32, name="word_table%d" % g, align_bytes=64) for g in range(PASSES)]
         window = sb.tile([P, U], F32, name="window", align_bytes=64)
         w2_rows = w2.rearrange("(g p j) n -> g p j n", g=PASSES, j=PACK)
 
         def load_scales(g):
-            for q in range(4):
+            for q in range(P // QUADRANT):
+                row = QUADRANT * q + SCALE_ROWS * g
                 nc.sync.dma_start(
-                    planes[g][32 * q + 4 * g : 32 * q + 4 * g + 4, :].bitcast(I32),
-                    x_scales[g, 4 * q : 4 * q + 4, :].bitcast(I32),
+                    scale_table[g][row : row + SCALE_ROWS, :].bitcast(I32),
+                    x_scales[g, SCALE_ROWS * q : SCALE_ROWS * (q + 1), :].bitcast(I32),
                 )
 
         def load_words(g):
-            nc.sync.dma_start(table[g][:].bitcast(I32), x_words[g].rearrange("p n t -> p (n t)").bitcast(I32))
+            nc.sync.dma_start(word_table[g][:].bitcast(I32), x_words[g].rearrange("p n t -> p (n t)").bitcast(I32))
 
-        nc.sync.dma_start(raw1[:], w1.rearrange("(g p j) n -> p g j n", g=PASSES, j=PACK))
+        nc.sync.dma_start(w1_raw[:], w1.rearrange("(g p j) n -> p g j n", g=PASSES, j=PACK))
         nc.sync.dma_start(offs_t[:], offs)
         load_scales(0)
-        nc.sync.dma_start(raw2[0][:], w2_rows[0])
+        nc.sync.dma_start(w2_raw[0][:], w2_rows[0])
         load_words(0)
         load_scales(1)
         load_words(1)
-        nc.sync.dma_start(raw2[1][:], w2_rows[1])
+        nc.sync.dma_start(w2_raw[1][:], w2_rows[1])
         nc.sync.dma_start(slot_t[:], slot)
         nc.sync.dma_start(window[:], mem)
-        nc.scalar.activation(warm_out[:], warm_in[:], ACT.Sigmoid)
 
-        grouped1 = sb.tile([P, PASSES, N, PACK], BF16, name="grouped1", align_bytes=64)
-        nc.vector.tensor_copy(grouped1[:], raw1[:].rearrange("p g j n -> p g n j"))
-        codes1 = sb.tile([P, PASSES * N], U32, name="codes1", align_bytes=64)
-        scales1 = sb.tile([P, PASSES * N], U8, name="scales1", align_bytes=64)
+        w1_bf16 = sb.tile([P, PASSES, N, PACK], BF16, name="w1_bf16", align_bytes=64)
+        nc.vector.tensor_copy(w1_bf16[:], w1_raw[:].rearrange("p g j n -> p g n j"))
+        w1_words = sb.tile([P, PASSES * N], U32, name="w1_words", align_bytes=64)
+        w1_scales = sb.tile([P, PASSES * N], U8, name="w1_scales", align_bytes=64)
         nc.vector.quantize_mx(
-            out=codes1[:].bitcast(FP8X4), scales=scales1[:], in_=grouped1[:].rearrange("p g n j -> p (g n j)")
+            out=w1_words[:].bitcast(FP8X4), scales=w1_scales[:], in_=w1_bf16[:].rearrange("p g n j -> p (g n j)")
         )
-        codes = [[codes1[:, g * N : (g + 1) * N] for g in range(PASSES)], []]
-        scales = [[scales1[:, g * N : (g + 1) * N] for g in range(PASSES)], []]
+        weights = {
+            (CANDIDATE, g): (w1_words[:, g * N : (g + 1) * N], w1_scales[:, g * N : (g + 1) * N])
+            for g in range(PASSES)
+        }
 
         def quantise_gate(g):
-            grouped = sb.tile([P, N, PACK], BF16, name="grouped2_%d" % g, align_bytes=64)
-            nc.scalar.copy(grouped[:], raw2[g][:].rearrange("p j n -> p n j"))
-            c = sb.tile([P, N], U32, name="codes2_%d" % g, align_bytes=64)
-            s = sb.tile([P, N], U8, name="scales2_%d" % g, align_bytes=64)
+            w2_bf16 = sb.tile([P, N, PACK], BF16, name="w2_bf16_%d" % g, align_bytes=64)
+            nc.scalar.copy(w2_bf16[:], w2_raw[g][:].rearrange("p j n -> p n j"))
+            w2_words = sb.tile([P, N], U32, name="w2_words%d" % g, align_bytes=64)
+            w2_scales = sb.tile([P, N], U8, name="w2_scales%d" % g, align_bytes=64)
             nc.vector.quantize_mx(
-                out=c[:].bitcast(FP8X4), scales=s[:], in_=grouped[:].rearrange("p n j -> p (n j)")
+                out=w2_words[:].bitcast(FP8X4), scales=w2_scales[:], in_=w2_bf16[:].rearrange("p n j -> p (n j)")
             )
-            codes[1].append(c[:])
-            scales[1].append(s[:])
+            weights[GATE, g] = (w2_words[:], w2_scales[:])
 
         quantise_gate(0)
-        x_planes = [sb.tile([P, S], U8, name="x_planes%d" % g, align_bytes=64) for g in range(PASSES)]
-        nc.vector.tensor_copy(x_planes[0][:], planes[0][:].indirect(offs_t[:]))
-        first = sb.tile([P, S], U32, name="first", align_bytes=64)
-        nc.vector.tensor_copy(first[:], table[0][:].indirect(offs_t[:]))
-        nc.vector.tensor_copy(x_planes[1][:], planes[1][:].indirect(offs_t[:]))
 
-        acc = [[ps.tile([P, 512], F32, name="acc%d_%d" % (h, i)) for i in range(2)] for h in range(2)]
+        picked_scales = [sb.tile([P, S], U8, name="picked_scales%d" % g, align_bytes=64) for g in range(PASSES)]
+        nc.vector.tensor_copy(picked_scales[0][:], scale_table[0][:].indirect(offs_t[:]))
+        first_words = sb.tile([P, S], U32, name="first_words", align_bytes=64)
+        nc.vector.tensor_copy(first_words[:], word_table[0][:].indirect(offs_t[:]))
+        nc.vector.tensor_copy(picked_scales[1][:], scale_table[1][:].indirect(offs_t[:]))
 
-        def product(h, i, g, words):
+        acc = [
+            [ps.tile([P, BANK], F32, name="acc%d_%d" % (h, product)) for product in (CANDIDATE, GATE)]
+            for h in range(HALVES)
+        ]
+        cols = [slice(h * HALF, (h + 1) * HALF) for h in range(HALVES)]
+        list_cols = [slice(h * HALF // LIST_ROWS, (h + 1) * HALF // LIST_ROWS) for h in range(HALVES)]
+
+        def multiply(h, product, g, picked_words):
+            w_words, w_scales = weights[product, g]
             nc.tensor.matmul_mx(
-                out=acc[h][i][:, :HALF],
-                lhsT=codes[i][g].bitcast(FP8X4),
-                lhsT_scale=scales[i][g],
-                rhs=words.bitcast(FP8X4),
-                rhs_scale=x_planes[g][4 * g :, h * HALF : (h + 1) * HALF],
+                out=acc[h][product][:, :HALF],
+                lhsT=w_words.bitcast(FP8X4),
+                lhsT_scale=w_scales,
+                rhs=picked_words.bitcast(FP8X4),
+                rhs_scale=picked_scales[g][SCALE_ROWS * g :, cols[h]],
                 start=(g == 0),
                 stop=(g == PASSES - 1),
             )
 
-        for h in range(2):
-            for i in range(2):
-                product(h, i, 0, first[:, h * HALF : (h + 1) * HALF])
+        for h in range(HALVES):
+            for product in (CANDIDATE, GATE):
+                multiply(h, product, 0, first_words[:, cols[h]])
 
         cand = sb.tile([P, S], F32, name="cand", align_bytes=64)
+        gate_tanh = sb.tile([P, S], F32, name="gate_tanh", align_bytes=64)
         keep = sb.tile([P, S], F32, name="keep", align_bytes=64)
         diff = sb.tile([P, S], F32, name="diff", align_bytes=64)
-        rest = sb.tile([P, S], F32, name="rest", align_bytes=64)
-        cols = [slice(h * HALF, (h + 1) * HALF) for h in range(2)]
-        lcols = [slice(h * HALF // LANES, (h + 1) * HALF // LANES) for h in range(2)]
-        second = [sb.tile([P, HALF], U32, name="second%d" % h, align_bytes=64) for h in range(2)]
-        for h in range(2):
-            nc.vector.tensor_copy(second[h][:], table[1][:].indirect(offs_t[:, lcols[h]]))
-            product(h, 0, 1, second[h][:])
+        kept = sb.tile([P, S], F32, name="kept", align_bytes=64)
+
+        last_words = [sb.tile([P, HALF], U32, name="last_words%d" % h, align_bytes=64) for h in range(HALVES)]
+        for h in range(HALVES):
+            nc.vector.tensor_copy(last_words[h][:], word_table[1][:].indirect(offs_t[:, list_cols[h]]))
+            multiply(h, CANDIDATE, 1, last_words[h][:])
         quantise_gate(1)
-        for h in range(2):
-            nc.scalar.activation(cand[:, cols[h]], acc[h][0][:, :HALF], ACT.Tanh)
-        for h in range(2):
-            product(h, 1, 1, second[h][:])
-            nc.scalar.activation(keep[:, cols[h]], acc[h][1][:, :HALF], ACT.Sigmoid, scale=-1.0)
-        for h in range(2):
+        for h in range(HALVES):
+            nc.scalar.activation(cand[:, cols[h]], acc[h][CANDIDATE][:, :HALF], ACT.Tanh)
+        for h in range(HALVES):
+            multiply(h, GATE, 1, last_words[h][:])
+            nc.scalar.activation(gate_tanh[:, cols[h]], acc[h][GATE][:, :HALF], ACT.Tanh, scale=0.5)
+            nc.scalar.activation(keep[:, cols[h]], gate_tanh[:, cols[h]], ACT.Copy, scale=-0.5, bias=0.5)
+
+        for h in range(HALVES):
             nc.vector.tensor_tensor(
-                diff[:, cols[h]], window[:].indirect(slot_t[:, lcols[h]]), cand[:, cols[h]], ALU.subtract
+                diff[:, cols[h]], window[:].indirect(slot_t[:, list_cols[h]]), cand[:, cols[h]], ALU.subtract
             )
-        for h in range(2):
-            nc.vector.tensor_tensor(rest[:, cols[h]], diff[:, cols[h]], keep[:, cols[h]], ALU.mult)
-        nc.vector.tensor_tensor(window[:].indirect(slot_t[:]), rest[:], cand[:], ALU.add)
+        for h in range(HALVES):
+            nc.vector.tensor_tensor(kept[:, cols[h]], diff[:, cols[h]], keep[:, cols[h]], ALU.mult)
+        nc.vector.tensor_tensor(window[:].indirect(slot_t[:]), kept[:], cand[:], ALU.add)
         nc.sync.dma_start(out, window[:])

@@ -39,6 +39,9 @@ def tile_picked_gmem_tanh_p_kernel(tc, x_words, x_scales, mem, w1, w2, offs, slo
         scale_table = [sb.tile([P, T], U8, name="scale_table%d" % g, align_bytes=64) for g in range(PASSES)]
         for g in range(PASSES):
             nc.vector.memset(scale_table[g][:].bitcast(I32), 0)
+        warm_in = sb.tile([P, 1], F32, name="warm_in")
+        warm_out = sb.tile([P, 1], F32, name="warm_out")
+        nc.vector.memset(warm_in[:], 0.0)
 
         w1_raw = sb.tile([P, PASSES, PACK, N], F32, name="w1_raw")
         w2_raw = [sb.tile([P, PACK, N], F32, name="w2_raw%d" % g) for g in range(PASSES)]
@@ -60,13 +63,14 @@ def tile_picked_gmem_tanh_p_kernel(tc, x_words, x_scales, mem, w1, w2, offs, slo
         nc.sync.dma_start(w1_raw[:], w1.rearrange("(g p j) n -> p g j n", g=PASSES, j=PACK))
         nc.sync.dma_start(offs_t[:], offs)
         load_scales(0)
-        nc.sync.dma_start(w2_raw[0][:], w2_rows[0])
         load_words(0)
         load_scales(1)
         load_words(1)
-        nc.sync.dma_start(w2_raw[1][:], w2_rows[1])
+        for g in range(PASSES):
+            nc.sync.dma_start(w2_raw[g][:], w2_rows[g])
         nc.sync.dma_start(slot_t[:], slot)
         nc.sync.dma_start(window[:], mem)
+        nc.scalar.activation(warm_out[:], warm_in[:], ACT.Sigmoid)
 
         w1_bf16 = sb.tile([P, PASSES, N, PACK], BF16, name="w1_bf16", align_bytes=64)
         nc.vector.tensor_copy(w1_bf16[:], w1_raw[:].rearrange("p g j n -> p g n j"))
@@ -80,17 +84,15 @@ def tile_picked_gmem_tanh_p_kernel(tc, x_words, x_scales, mem, w1, w2, offs, slo
             for g in range(PASSES)
         }
 
-        def quantise_gate(g):
+        def quantise_gate(g, round_and_interleave):
             w2_bf16 = sb.tile([P, N, PACK], BF16, name="w2_bf16_%d" % g, align_bytes=64)
-            nc.scalar.copy(w2_bf16[:], w2_raw[g][:].rearrange("p j n -> p n j"))
+            round_and_interleave(w2_bf16[:], w2_raw[g][:].rearrange("p j n -> p n j"))
             w2_words = sb.tile([P, N], U32, name="w2_words%d" % g, align_bytes=64)
             w2_scales = sb.tile([P, N], U8, name="w2_scales%d" % g, align_bytes=64)
             nc.vector.quantize_mx(
                 out=w2_words[:].bitcast(FP8X4), scales=w2_scales[:], in_=w2_bf16[:].rearrange("p n j -> p (n j)")
             )
             weights[GATE, g] = (w2_words[:], w2_scales[:])
-
-        quantise_gate(0)
 
         picked_scales = [sb.tile([P, S], U8, name="picked_scales%d" % g, align_bytes=64) for g in range(PASSES)]
         nc.vector.tensor_copy(picked_scales[0][:], scale_table[0][:].indirect(offs_t[:]))
@@ -118,11 +120,9 @@ def tile_picked_gmem_tanh_p_kernel(tc, x_words, x_scales, mem, w1, w2, offs, slo
             )
 
         for h in range(HALVES):
-            for product in (CANDIDATE, GATE):
-                multiply(h, product, 0, first_words[:, cols[h]])
+            multiply(h, CANDIDATE, 0, first_words[:, cols[h]])
 
         cand = sb.tile([P, S], F32, name="cand", align_bytes=64)
-        gate_tanh = sb.tile([P, S], F32, name="gate_tanh", align_bytes=64)
         keep = sb.tile([P, S], F32, name="keep", align_bytes=64)
         diff = sb.tile([P, S], F32, name="diff", align_bytes=64)
         kept = sb.tile([P, S], F32, name="kept", align_bytes=64)
@@ -131,13 +131,15 @@ def tile_picked_gmem_tanh_p_kernel(tc, x_words, x_scales, mem, w1, w2, offs, slo
         for h in range(HALVES):
             nc.vector.tensor_copy(last_words[h][:], word_table[1][:].indirect(offs_t[:, list_cols[h]]))
             multiply(h, CANDIDATE, 1, last_words[h][:])
-        quantise_gate(1)
+        quantise_gate(0, nc.scalar.copy)
+        quantise_gate(1, nc.vector.tensor_copy)
         for h in range(HALVES):
             nc.scalar.activation(cand[:, cols[h]], acc[h][CANDIDATE][:, :HALF], ACT.Tanh)
         for h in range(HALVES):
+            multiply(h, GATE, 0, first_words[:, cols[h]])
+        for h in range(HALVES):
             multiply(h, GATE, 1, last_words[h][:])
-            nc.scalar.activation(gate_tanh[:, cols[h]], acc[h][GATE][:, :HALF], ACT.Tanh, scale=0.5)
-            nc.scalar.activation(keep[:, cols[h]], gate_tanh[:, cols[h]], ACT.Copy, scale=-0.5, bias=0.5)
+            nc.scalar.activation(keep[:, cols[h]], acc[h][GATE][:, :HALF], ACT.Sigmoid, scale=-1.0)
 
         for h in range(HALVES):
             nc.vector.tensor_tensor(

@@ -36,9 +36,8 @@ def tile_picked_gmem_tanh_p_kernel(tc, x_words, x_scales, mem, w1, w2, offs, slo
         offs_t = sb.tile([P, S // LIST_ROWS], U16, name="offs_t")
         slot_t = sb.tile([P, S // LIST_ROWS], U16, name="slot_t")
 
-        scale_table = [sb.tile([P, T], U8, name="scale_table%d" % g, align_bytes=64) for g in range(PASSES)]
-        for g in range(PASSES):
-            nc.vector.memset(scale_table[g][:].bitcast(I32), 0)
+        scale_table = sb.tile([P, T], U8, name="scale_table", align_bytes=64)
+        nc.vector.memset(scale_table[:].bitcast(I32), 0)
         warm_in = sb.tile([P, 1], F32, name="warm_in")
         warm_out = sb.tile([P, 1], F32, name="warm_out")
         nc.vector.memset(warm_in[:], 0.0)
@@ -49,22 +48,22 @@ def tile_picked_gmem_tanh_p_kernel(tc, x_words, x_scales, mem, w1, w2, offs, slo
         window = sb.tile([P, U], F32, name="window", align_bytes=64)
         w2_rows = w2.rearrange("(g p j) n -> g p j n", g=PASSES, j=PACK)
 
-        def load_scales(g):
-            for q in range(P // QUADRANT):
-                row = QUADRANT * q + SCALE_ROWS * g
-                nc.sync.dma_start(
-                    scale_table[g][row : row + SCALE_ROWS, :].bitcast(I32),
-                    x_scales[g, SCALE_ROWS * q : SCALE_ROWS * (q + 1), :].bitcast(I32),
-                )
+        def load_scales(rows):
+            for r in rows:
+                for g in range(PASSES):
+                    nc.sync.dma_start(
+                        scale_table[SCALE_ROWS * g + r : P : QUADRANT, :].bitcast(I32),
+                        x_scales[g, r::SCALE_ROWS, :].bitcast(I32),
+                    )
 
         def load_words(g):
             nc.sync.dma_start(word_table[g][:].bitcast(I32), x_words[g].rearrange("p n t -> p (n t)").bitcast(I32))
 
         nc.sync.dma_start(w1_raw[:], w1.rearrange("(g p j) n -> p g j n", g=PASSES, j=PACK))
         nc.sync.dma_start(offs_t[:], offs)
-        load_scales(0)
+        load_scales(range(SCALE_ROWS // 2))
         load_words(0)
-        load_scales(1)
+        load_scales(range(SCALE_ROWS // 2, SCALE_ROWS))
         load_words(1)
         for g in range(PASSES):
             nc.sync.dma_start(w2_raw[g][:], w2_rows[g])
@@ -94,11 +93,10 @@ def tile_picked_gmem_tanh_p_kernel(tc, x_words, x_scales, mem, w1, w2, offs, slo
             )
             weights[GATE, g] = (w2_words[:], w2_scales[:])
 
-        picked_scales = [sb.tile([P, S], U8, name="picked_scales%d" % g, align_bytes=64) for g in range(PASSES)]
-        nc.vector.tensor_copy(picked_scales[0][:], scale_table[0][:].indirect(offs_t[:]))
+        picked_scales = sb.tile([P, S], U8, name="picked_scales", align_bytes=64)
         first_words = sb.tile([P, S], U32, name="first_words", align_bytes=64)
         nc.vector.tensor_copy(first_words[:], word_table[0][:].indirect(offs_t[:]))
-        nc.vector.tensor_copy(picked_scales[1][:], scale_table[1][:].indirect(offs_t[:]))
+        nc.vector.tensor_copy(picked_scales[:], scale_table[:].indirect(offs_t[:]))
 
         acc = [
             [ps.tile([P, BANK], F32, name="acc%d_%d" % (h, product)) for product in (CANDIDATE, GATE)]
@@ -114,7 +112,7 @@ def tile_picked_gmem_tanh_p_kernel(tc, x_words, x_scales, mem, w1, w2, offs, slo
                 lhsT=w_words.bitcast(FP8X4),
                 lhsT_scale=w_scales,
                 rhs=picked_words.bitcast(FP8X4),
-                rhs_scale=picked_scales[g][SCALE_ROWS * g :, cols[h]],
+                rhs_scale=picked_scales[SCALE_ROWS * g :, cols[h]],
                 start=(g == 0),
                 stop=(g == PASSES - 1),
             )

@@ -21,6 +21,8 @@ PASSES = K // (P * PACK)
 QUADRANT = 32
 SCALE_ROWS = 4
 LIST_ROWS = 16
+LINE = 4
+DMA_ALIGN = 256
 BANK = 512
 HALVES = 2
 HALF = S // HALVES
@@ -36,16 +38,16 @@ def tile_picked_gmem_tanh_p_kernel(tc, x_words, x_scales, mem, w1, w2, offs, slo
         offs_t = sb.tile([P, S // LIST_ROWS], U16, name="offs_t")
         slot_t = sb.tile([P, S // LIST_ROWS], U16, name="slot_t")
 
-        scale_table = sb.tile([P, T], U8, name="scale_table", align_bytes=64)
+        scale_table = sb.tile([P, T], U8, name="scale_table", align_bytes=DMA_ALIGN)
         nc.vector.memset(scale_table[:].bitcast(I32), 0)
         warm_in = sb.tile([P, 1], F32, name="warm_in")
         warm_out = sb.tile([P, 1], F32, name="warm_out")
         nc.vector.memset(warm_in[:], 0.0)
 
-        w1_raw = sb.tile([P, PASSES, PACK, N], F32, name="w1_raw")
-        w2_raw = [sb.tile([P, PACK, N], F32, name="w2_raw%d" % g) for g in range(PASSES)]
-        word_table = [sb.tile([P, T], U32, name="word_table%d" % g, align_bytes=64) for g in range(PASSES)]
-        window = sb.tile([P, U], F32, name="window", align_bytes=64)
+        w1_raw = sb.tile([P, PASSES, PACK, N], F32, name="w1_raw", align_bytes=DMA_ALIGN)
+        w2_raw = [sb.tile([P, PACK, N], F32, name="w2_raw%d" % g, align_bytes=DMA_ALIGN) for g in range(PASSES)]
+        word_table = [sb.tile([P, T], U32, name="word_table%d" % g, align_bytes=DMA_ALIGN) for g in range(PASSES)]
+        window = sb.tile([P, U], F32, name="window", align_bytes=DMA_ALIGN)
         w2_rows = w2.rearrange("(g p j) n -> g p j n", g=PASSES, j=PACK)
 
         def load_scales(rows):
@@ -72,7 +74,9 @@ def tile_picked_gmem_tanh_p_kernel(tc, x_words, x_scales, mem, w1, w2, offs, slo
         nc.scalar.activation(warm_out[:], warm_in[:], ACT.Sigmoid)
 
         w1_bf16 = sb.tile([P, PASSES, N, PACK], BF16, name="w1_bf16", align_bytes=64)
-        nc.vector.tensor_copy(w1_bf16[:], w1_raw[:].rearrange("p g j n -> p g n j"))
+        nc.vector.tensor_copy(
+            w1_bf16[:].rearrange("p g (c i) j -> p g c j i", i=LINE), w1_raw[:].rearrange("p g j (c i) -> p g c j i", i=LINE)
+        )
         w1_words = sb.tile([P, PASSES * N], U32, name="w1_words", align_bytes=64)
         w1_scales = sb.tile([P, PASSES * N], U8, name="w1_scales", align_bytes=64)
         nc.vector.quantize_mx(
@@ -85,7 +89,9 @@ def tile_picked_gmem_tanh_p_kernel(tc, x_words, x_scales, mem, w1, w2, offs, slo
 
         def quantise_gate(g, round_and_interleave):
             w2_bf16 = sb.tile([P, N, PACK], BF16, name="w2_bf16_%d" % g, align_bytes=64)
-            round_and_interleave(w2_bf16[:], w2_raw[g][:].rearrange("p j n -> p n j"))
+            round_and_interleave(
+                w2_bf16[:].rearrange("p (c i) j -> p c j i", i=LINE), w2_raw[g][:].rearrange("p j (c i) -> p c j i", i=LINE)
+            )
             w2_words = sb.tile([P, N], U32, name="w2_words%d" % g, align_bytes=64)
             w2_scales = sb.tile([P, N], U8, name="w2_scales%d" % g, align_bytes=64)
             nc.vector.quantize_mx(

@@ -40,6 +40,8 @@ def tile_picked_gmem_tanh_p_kernel(tc, x_words, x_scales, mem, w1, w2, offs, slo
 
         scale_table = sb.tile([P, T], U8, name="scale_table", align_bytes=DMA_ALIGN)
         nc.vector.memset(scale_table[:].bitcast(I32), 0)
+        planes = sb.tile([P, PASSES, S], U8, name="planes", align_bytes=DMA_ALIGN)
+        nc.vector.memset(planes[:].rearrange("p g s -> p (g s)").bitcast(I32), 0)
         warm_in = sb.tile([P, 1], F32, name="warm_in")
         warm_out = sb.tile([P, 1], F32, name="warm_out")
         nc.vector.memset(warm_in[:], 0.0)
@@ -50,26 +52,21 @@ def tile_picked_gmem_tanh_p_kernel(tc, x_words, x_scales, mem, w1, w2, offs, slo
         window = sb.tile([P, U], F32, name="window", align_bytes=DMA_ALIGN)
         w2_rows = w2.rearrange("(g p j) n -> g p j n", g=PASSES, j=PACK)
 
-        def load_scales(rows):
-            for r in rows:
-                for g in range(PASSES):
-                    nc.sync.dma_start(
-                        scale_table[SCALE_ROWS * g + r : P : QUADRANT, :].bitcast(I32),
-                        x_scales[g, r::SCALE_ROWS, :].bitcast(I32),
-                    )
+        def load_scales(g):
+            nc.sync.dma_start(scale_table[SCALE_ROWS * g : P : 2 * SCALE_ROWS, :].bitcast(I32), x_scales[g].bitcast(I32))
 
         def load_words(g):
             nc.sync.dma_start(word_table[g][:].bitcast(I32), x_words[g].rearrange("p n t -> p (n t)").bitcast(I32))
 
         nc.sync.dma_start(w1_raw[:], w1.rearrange("(g p j) n -> p g j n", g=PASSES, j=PACK))
         nc.sync.dma_start(offs_t[:], offs)
-        load_scales(range(SCALE_ROWS // 2))
-        load_words(0)
-        load_scales(range(SCALE_ROWS // 2, SCALE_ROWS))
-        load_words(1)
+        nc.sync.dma_start(slot_t[:], slot)
+        for g in range(PASSES):
+            load_scales(g)
+        for g in range(PASSES):
+            load_words(g)
         for g in range(PASSES):
             nc.sync.dma_start(w2_raw[g][:], w2_rows[g])
-        nc.sync.dma_start(slot_t[:], slot)
         nc.sync.dma_start(window[:], mem)
         nc.scalar.activation(warm_out[:], warm_in[:], ACT.Sigmoid)
 
@@ -99,10 +96,15 @@ def tile_picked_gmem_tanh_p_kernel(tc, x_words, x_scales, mem, w1, w2, offs, slo
             )
             weights[GATE, g] = (w2_words[:], w2_scales[:])
 
-        picked_scales = sb.tile([P, S], U8, name="picked_scales", align_bytes=64)
+        picked_scales = sb.tile([P, S], U8, name="picked_scales", align_bytes=DMA_ALIGN)
+        nc.vector.tensor_copy(picked_scales[:], scale_table[:].indirect(offs_t[:]))
+        for q in range(P // QUADRANT):
+            nc.scalar.dma_start(
+                planes[QUADRANT * q : QUADRANT * q + SCALE_ROWS].rearrange("p g s -> p (g s)").bitcast(I32),
+                picked_scales[QUADRANT * q : QUADRANT * (q + 1) : SCALE_ROWS, :].bitcast(I32),
+            )
         first_words = sb.tile([P, S], U32, name="first_words", align_bytes=64)
         nc.vector.tensor_copy(first_words[:], word_table[0][:].indirect(offs_t[:]))
-        nc.vector.tensor_copy(picked_scales[:], scale_table[:].indirect(offs_t[:]))
 
         acc = [
             [ps.tile([P, BANK], F32, name="acc%d_%d" % (h, product)) for product in (CANDIDATE, GATE)]
@@ -118,7 +120,7 @@ def tile_picked_gmem_tanh_p_kernel(tc, x_words, x_scales, mem, w1, w2, offs, slo
                 lhsT=w_words.bitcast(FP8X4),
                 lhsT_scale=w_scales,
                 rhs=picked_words.bitcast(FP8X4),
-                rhs_scale=picked_scales[SCALE_ROWS * g :, cols[h]],
+                rhs_scale=planes[:, g, cols[h]],
                 start=(g == 0),
                 stop=(g == PASSES - 1),
             )

@@ -33,12 +33,13 @@ def tile_picked_gmem_tanh_p_kernel(tc, x_words, x_scales, mem, w1, w2, offs, slo
     nc = tc.nc
     with ExitStack() as ctx:
         sb = ctx.enter_context(tc.tile_pool(name="sb", bufs=1))
+        shared = ctx.enter_context(tc.tile_pool(name="shared", bufs=1))
         ps = ctx.enter_context(tc.psum_pool(name="ps", bufs=1))
 
         offs_t = sb.tile([P, S // LIST_ROWS], U16, name="offs_t")
         slot_t = sb.tile([P, S // LIST_ROWS], U16, name="slot_t")
 
-        scale_table = sb.tile([P, T], U8, name="scale_table", align_bytes=DMA_ALIGN)
+        scale_table = shared.tile([P, T], U8, name="scale_table", align_bytes=DMA_ALIGN, offset=1792)
         nc.vector.memset(scale_table[:].bitcast(I32), 0)
         planes = sb.tile([P, PASSES, S], U8, name="planes", align_bytes=DMA_ALIGN)
         nc.vector.memset(planes[:].rearrange("p g s -> p (g s)").bitcast(I32), 0)
@@ -47,9 +48,7 @@ def tile_picked_gmem_tanh_p_kernel(tc, x_words, x_scales, mem, w1, w2, offs, slo
         nc.vector.memset(warm_in[:], 0.0)
 
         w1_raw = sb.tile([P, PASSES, PACK, N], F32, name="w1_raw", align_bytes=DMA_ALIGN)
-        w2_raw = [sb.tile([P, PACK, N], F32, name="w2_raw%d" % g, align_bytes=DMA_ALIGN) for g in range(PASSES)]
         word_table = [sb.tile([P, T], U32, name="word_table%d" % g, align_bytes=DMA_ALIGN) for g in range(PASSES)]
-        window = sb.tile([P, U], F32, name="window", align_bytes=DMA_ALIGN)
         w2_rows = w2.rearrange("(g p j) n -> g p j n", g=PASSES, j=PACK)
 
         def load_scales(g):
@@ -60,22 +59,26 @@ def tile_picked_gmem_tanh_p_kernel(tc, x_words, x_scales, mem, w1, w2, offs, slo
 
         nc.sync.dma_start(w1_raw[:], w1.rearrange("(g p j) n -> p g j n", g=PASSES, j=PACK))
         nc.sync.dma_start(offs_t[:], offs)
-        nc.sync.dma_start(slot_t[:], slot)
         for g in range(PASSES):
             load_scales(g)
+        nc.sync.dma_start(slot_t[:], slot)
         for g in range(PASSES):
             load_words(g)
-        for g in range(PASSES):
-            nc.sync.dma_start(w2_raw[g][:], w2_rows[g])
-        nc.sync.dma_start(window[:], mem)
         nc.scalar.activation(warm_out[:], warm_in[:], ACT.Sigmoid)
 
-        w1_bf16 = sb.tile([P, PASSES, N, PACK], BF16, name="w1_bf16", align_bytes=64)
-        nc.vector.tensor_copy(
+        w1_bf16 = shared.tile([P, PASSES, N, PACK], BF16, name="w1_bf16", align_bytes=DMA_ALIGN, offset=5632)
+        nc.scalar.copy(
             w1_bf16[:].rearrange("p g (c i) j -> p g c j i", i=LINE), w1_raw[:].rearrange("p g j (c i) -> p g c j i", i=LINE)
         )
+        picked_scales = sb.tile([P, S], U8, name="picked_scales", align_bytes=DMA_ALIGN)
+        nc.vector.tensor_copy(picked_scales[:], scale_table[:].indirect(offs_t[:]))
+        for q in range(P // QUADRANT):
+            nc.sync.dma_start(
+                planes[QUADRANT * q : QUADRANT * q + SCALE_ROWS].rearrange("p g s -> p (g s)").bitcast(I32),
+                picked_scales[QUADRANT * q : QUADRANT * (q + 1) : SCALE_ROWS, :].bitcast(I32),
+            )
         w1_words = sb.tile([P, PASSES * N], U32, name="w1_words", align_bytes=64)
-        w1_scales = sb.tile([P, PASSES * N], U8, name="w1_scales", align_bytes=64)
+        w1_scales = shared.tile([P, PASSES * N], U8, name="w1_scales", align_bytes=DMA_ALIGN, offset=2048)
         nc.vector.quantize_mx(
             out=w1_words[:].bitcast(FP8X4), scales=w1_scales[:], in_=w1_bf16[:].rearrange("p g n j -> p (g n j)")
         )
@@ -96,15 +99,16 @@ def tile_picked_gmem_tanh_p_kernel(tc, x_words, x_scales, mem, w1, w2, offs, slo
             )
             weights[GATE, g] = (w2_words[:], w2_scales[:])
 
-        picked_scales = sb.tile([P, S], U8, name="picked_scales", align_bytes=DMA_ALIGN)
-        nc.vector.tensor_copy(picked_scales[:], scale_table[:].indirect(offs_t[:]))
-        for q in range(P // QUADRANT):
-            nc.scalar.dma_start(
-                planes[QUADRANT * q : QUADRANT * q + SCALE_ROWS].rearrange("p g s -> p (g s)").bitcast(I32),
-                picked_scales[QUADRANT * q : QUADRANT * (q + 1) : SCALE_ROWS, :].bitcast(I32),
-            )
         first_words = sb.tile([P, S], U32, name="first_words", align_bytes=64)
         nc.vector.tensor_copy(first_words[:], word_table[0][:].indirect(offs_t[:]))
+        w2_raw = [
+            shared.tile([P, PACK, N], F32, name="w2_raw%d" % g, align_bytes=DMA_ALIGN, offset=3584 * g)
+            for g in range(PASSES)
+        ]
+        for g in range(PASSES):
+            nc.sync.dma_start(w2_raw[g][:], w2_rows[g])
+        window = shared.tile([P, U], F32, name="window", align_bytes=DMA_ALIGN, offset=5632)
+        nc.sync.dma_start(window[:], mem)
 
         acc = [
             [ps.tile([P, BANK], F32, name="acc%d_%d" % (h, product)) for product in (CANDIDATE, GATE)]
@@ -128,7 +132,7 @@ def tile_picked_gmem_tanh_p_kernel(tc, x_words, x_scales, mem, w1, w2, offs, slo
         for h in range(HALVES):
             multiply(h, CANDIDATE, 0, first_words[:, cols[h]])
 
-        cand = sb.tile([P, S], F32, name="cand", align_bytes=64)
+        cand = shared.tile([P, S], F32, name="cand", align_bytes=DMA_ALIGN, offset=0)
         keep = sb.tile([P, S], F32, name="keep", align_bytes=64)
         diff = sb.tile([P, S], F32, name="diff", align_bytes=64)
         kept = sb.tile([P, S], F32, name="kept", align_bytes=64)

@@ -20,13 +20,23 @@ PACK = 4
 PASSES = K // (P * PACK)
 QUADRANT = 32
 SCALE_ROWS = 4
+SPREAD = QUADRANT // (SCALE_ROWS * PASSES)
 LIST_ROWS = 16
 LINE = 4
+MX_ALIGN = 64
 DMA_ALIGN = 256
 BANK = 512
 HALVES = 2
 HALF = S // HALVES
 CANDIDATE, GATE = 0, 1
+
+RAW_PASS_BYTES = PACK * N * 4
+W2_RAW_AT = (0, RAW_PASS_BYTES + T - 2 * DMA_ALIGN)
+SCALE_TABLE_AT = RAW_PASS_BYTES - DMA_ALIGN
+W1_SCALES_AT = RAW_PASS_BYTES
+CAND_AT = W2_RAW_AT[0]
+W1_BF16_AT = W2_RAW_AT[1] + RAW_PASS_BYTES
+WINDOW_AT = W1_BF16_AT
 
 
 def tile_picked_gmem_tanh_p_kernel(tc, x_words, x_scales, mem, w1, w2, offs, slot, out):
@@ -39,46 +49,42 @@ def tile_picked_gmem_tanh_p_kernel(tc, x_words, x_scales, mem, w1, w2, offs, slo
         offs_t = sb.tile([P, S // LIST_ROWS], U16, name="offs_t")
         slot_t = sb.tile([P, S // LIST_ROWS], U16, name="slot_t")
 
-        scale_table = shared.tile([P, T], U8, name="scale_table", align_bytes=DMA_ALIGN, offset=1792)
+        scale_table = shared.tile([P, T], U8, name="scale_table", align_bytes=DMA_ALIGN, offset=SCALE_TABLE_AT)
         nc.vector.memset(scale_table[:].bitcast(I32), 0)
-        planes = sb.tile([P, PASSES, S], U8, name="planes", align_bytes=DMA_ALIGN)
-        nc.vector.memset(planes[:].rearrange("p g s -> p (g s)").bitcast(I32), 0)
+        placed_scales = sb.tile([P, PASSES, S], U8, name="placed_scales", align_bytes=DMA_ALIGN)
+        nc.vector.memset(placed_scales[:].rearrange("p g s -> p (g s)").bitcast(I32), 0)
         warm_in = sb.tile([P, 1], F32, name="warm_in")
         warm_out = sb.tile([P, 1], F32, name="warm_out")
         nc.vector.memset(warm_in[:], 0.0)
 
         w1_raw = sb.tile([P, PASSES, PACK, N], F32, name="w1_raw", align_bytes=DMA_ALIGN)
-        word_table = [sb.tile([P, T], U32, name="word_table%d" % g, align_bytes=DMA_ALIGN) for g in range(PASSES)]
-        w2_rows = w2.rearrange("(g p j) n -> g p j n", g=PASSES, j=PACK)
-
-        def load_scales(g):
-            nc.sync.dma_start(scale_table[SCALE_ROWS * g : P : 2 * SCALE_ROWS, :].bitcast(I32), x_scales[g].bitcast(I32))
-
-        def load_words(g):
-            nc.sync.dma_start(word_table[g][:].bitcast(I32), x_words[g].rearrange("p n t -> p (n t)").bitcast(I32))
-
         nc.sync.dma_start(w1_raw[:], w1.rearrange("(g p j) n -> p g j n", g=PASSES, j=PACK))
         nc.sync.dma_start(offs_t[:], offs)
-        for g in range(PASSES):
-            load_scales(g)
         nc.sync.dma_start(slot_t[:], slot)
+        nc.sync.dma_start(
+            scale_table[0:P:SPREAD, :].bitcast(I32), x_scales.rearrange("g row n -> row g n").bitcast(I32)
+        )
+        word_table = [sb.tile([P, T], U32, name="word_table%d" % g, align_bytes=DMA_ALIGN) for g in range(PASSES)]
         for g in range(PASSES):
-            load_words(g)
+            nc.sync.dma_start(word_table[g][:].bitcast(I32), x_words[g].rearrange("p n t -> p (n t)").bitcast(I32))
         nc.scalar.activation(warm_out[:], warm_in[:], ACT.Sigmoid)
 
-        w1_bf16 = shared.tile([P, PASSES, N, PACK], BF16, name="w1_bf16", align_bytes=DMA_ALIGN, offset=5632)
+        w1_bf16 = shared.tile([P, PASSES, N, PACK], BF16, name="w1_bf16", align_bytes=DMA_ALIGN, offset=W1_BF16_AT)
         nc.scalar.copy(
-            w1_bf16[:].rearrange("p g (c i) j -> p g c j i", i=LINE), w1_raw[:].rearrange("p g j (c i) -> p g c j i", i=LINE)
+            w1_bf16[:].rearrange("p g (c i) j -> p g c j i", i=LINE),
+            w1_raw[:].rearrange("p g j (c i) -> p g c j i", i=LINE),
         )
+
         picked_scales = sb.tile([P, S], U8, name="picked_scales", align_bytes=DMA_ALIGN)
         nc.vector.tensor_copy(picked_scales[:], scale_table[:].indirect(offs_t[:]))
-        for q in range(P // QUADRANT):
+        for first in (0, P // 2, QUADRANT, P // 2 + QUADRANT):
             nc.sync.dma_start(
-                planes[QUADRANT * q : QUADRANT * q + SCALE_ROWS].rearrange("p g s -> p (g s)").bitcast(I32),
-                picked_scales[QUADRANT * q : QUADRANT * (q + 1) : SCALE_ROWS, :].bitcast(I32),
+                placed_scales[first : first + SCALE_ROWS].rearrange("p g s -> p (g s)").bitcast(I32),
+                picked_scales[first : first + QUADRANT : SPREAD, :].bitcast(I32),
             )
-        w1_words = sb.tile([P, PASSES * N], U32, name="w1_words", align_bytes=64)
-        w1_scales = shared.tile([P, PASSES * N], U8, name="w1_scales", align_bytes=DMA_ALIGN, offset=2048)
+
+        w1_words = sb.tile([P, PASSES * N], U32, name="w1_words", align_bytes=MX_ALIGN)
+        w1_scales = shared.tile([P, PASSES * N], U8, name="w1_scales", align_bytes=DMA_ALIGN, offset=W1_SCALES_AT)
         nc.vector.quantize_mx(
             out=w1_words[:].bitcast(FP8X4), scales=w1_scales[:], in_=w1_bf16[:].rearrange("p g n j -> p (g n j)")
         )
@@ -87,28 +93,31 @@ def tile_picked_gmem_tanh_p_kernel(tc, x_words, x_scales, mem, w1, w2, offs, slo
             for g in range(PASSES)
         }
 
-        def quantise_gate(g, round_and_interleave):
-            w2_bf16 = sb.tile([P, N, PACK], BF16, name="w2_bf16_%d" % g, align_bytes=64)
-            round_and_interleave(
-                w2_bf16[:].rearrange("p (c i) j -> p c j i", i=LINE), w2_raw[g][:].rearrange("p j (c i) -> p c j i", i=LINE)
-            )
-            w2_words = sb.tile([P, N], U32, name="w2_words%d" % g, align_bytes=64)
-            w2_scales = sb.tile([P, N], U8, name="w2_scales%d" % g, align_bytes=64)
-            nc.vector.quantize_mx(
-                out=w2_words[:].bitcast(FP8X4), scales=w2_scales[:], in_=w2_bf16[:].rearrange("p n j -> p (n j)")
-            )
-            weights[GATE, g] = (w2_words[:], w2_scales[:])
-
-        first_words = sb.tile([P, S], U32, name="first_words", align_bytes=64)
+        first_words = sb.tile([P, S], U32, name="first_words", align_bytes=MX_ALIGN)
         nc.vector.tensor_copy(first_words[:], word_table[0][:].indirect(offs_t[:]))
+
+        w2_rows = w2.rearrange("(g p j) n -> g p j n", g=PASSES, j=PACK)
         w2_raw = [
-            shared.tile([P, PACK, N], F32, name="w2_raw%d" % g, align_bytes=DMA_ALIGN, offset=3584 * g)
+            shared.tile([P, PACK, N], F32, name="w2_raw%d" % g, align_bytes=DMA_ALIGN, offset=W2_RAW_AT[g])
             for g in range(PASSES)
         ]
         for g in range(PASSES):
             nc.sync.dma_start(w2_raw[g][:], w2_rows[g])
-        window = shared.tile([P, U], F32, name="window", align_bytes=DMA_ALIGN, offset=5632)
+        window = shared.tile([P, U], F32, name="window", align_bytes=DMA_ALIGN, offset=WINDOW_AT)
         nc.sync.dma_start(window[:], mem)
+
+        def quantise_gate(g, round_and_interleave):
+            w2_bf16 = sb.tile([P, N, PACK], BF16, name="w2_bf16_%d" % g, align_bytes=MX_ALIGN)
+            round_and_interleave(
+                w2_bf16[:].rearrange("p (c i) j -> p c j i", i=LINE),
+                w2_raw[g][:].rearrange("p j (c i) -> p c j i", i=LINE),
+            )
+            w2_words = sb.tile([P, N], U32, name="w2_words%d" % g, align_bytes=MX_ALIGN)
+            w2_scales = sb.tile([P, N], U8, name="w2_scales%d" % g, align_bytes=MX_ALIGN)
+            nc.vector.quantize_mx(
+                out=w2_words[:].bitcast(FP8X4), scales=w2_scales[:], in_=w2_bf16[:].rearrange("p n j -> p (n j)")
+            )
+            weights[GATE, g] = (w2_words[:], w2_scales[:])
 
         acc = [
             [ps.tile([P, BANK], F32, name="acc%d_%d" % (h, product)) for product in (CANDIDATE, GATE)]
@@ -124,7 +133,7 @@ def tile_picked_gmem_tanh_p_kernel(tc, x_words, x_scales, mem, w1, w2, offs, slo
                 lhsT=w_words.bitcast(FP8X4),
                 lhsT_scale=w_scales,
                 rhs=picked_words.bitcast(FP8X4),
-                rhs_scale=planes[:, g, cols[h]],
+                rhs_scale=placed_scales[:, g, cols[h]],
                 start=(g == 0),
                 stop=(g == PASSES - 1),
             )
@@ -132,12 +141,12 @@ def tile_picked_gmem_tanh_p_kernel(tc, x_words, x_scales, mem, w1, w2, offs, slo
         for h in range(HALVES):
             multiply(h, CANDIDATE, 0, first_words[:, cols[h]])
 
-        cand = shared.tile([P, S], F32, name="cand", align_bytes=DMA_ALIGN, offset=0)
-        keep = sb.tile([P, S], F32, name="keep", align_bytes=64)
-        diff = sb.tile([P, S], F32, name="diff", align_bytes=64)
-        kept = sb.tile([P, S], F32, name="kept", align_bytes=64)
+        cand = shared.tile([P, S], F32, name="cand", align_bytes=DMA_ALIGN, offset=CAND_AT)
+        keep = sb.tile([P, S], F32, name="keep", align_bytes=MX_ALIGN)
+        diff = sb.tile([P, S], F32, name="diff", align_bytes=MX_ALIGN)
+        kept = sb.tile([P, S], F32, name="kept", align_bytes=MX_ALIGN)
 
-        last_words = [sb.tile([P, HALF], U32, name="last_words%d" % h, align_bytes=64) for h in range(HALVES)]
+        last_words = [sb.tile([P, HALF], U32, name="last_words%d" % h, align_bytes=MX_ALIGN) for h in range(HALVES)]
         for h in range(HALVES):
             nc.vector.tensor_copy(last_words[h][:], word_table[1][:].indirect(offs_t[:, list_cols[h]]))
             multiply(h, CANDIDATE, 1, last_words[h][:])

@@ -28,15 +28,14 @@ DMA_ALIGN = 256
 BANK = 512
 HALVES = 2
 HALF = S // HALVES
-CANDIDATE, GATE = 0, 1
 
 RAW_PASS_BYTES = PACK * N * 4
-W2_RAW_AT = (0, RAW_PASS_BYTES + T - 2 * DMA_ALIGN)
+LATE_RAW_AT = (0, RAW_PASS_BYTES + T - 2 * DMA_ALIGN)
 SCALE_TABLE_AT = RAW_PASS_BYTES - DMA_ALIGN
-W1_SCALES_AT = RAW_PASS_BYTES
-CAND_AT = W2_RAW_AT[0]
-W1_BF16_AT = W2_RAW_AT[1] + RAW_PASS_BYTES
-WINDOW_AT = W1_BF16_AT
+EARLY_SCALES_AT = RAW_PASS_BYTES
+KEEP_AT = LATE_RAW_AT[0]
+EARLY_BF16_AT = LATE_RAW_AT[1] + RAW_PASS_BYTES
+WINDOW_AT = EARLY_BF16_AT
 
 
 def tile_picked_gmem_tanh_p_kernel(tc, x_words, x_scales, mem, w1, w2, offs, slot, out):
@@ -48,6 +47,8 @@ def tile_picked_gmem_tanh_p_kernel(tc, x_words, x_scales, mem, w1, w2, offs, slo
 
         offs_t = sb.tile([P, S // LIST_ROWS], U16, name="offs_t")
         slot_t = sb.tile([P, S // LIST_ROWS], U16, name="slot_t")
+        cols = [slice(h * HALF, (h + 1) * HALF) for h in range(HALVES)]
+        list_cols = [slice(h * HALF // LIST_ROWS, (h + 1) * HALF // LIST_ROWS) for h in range(HALVES)]
 
         scale_table = shared.tile([P, T], U8, name="scale_table", align_bytes=DMA_ALIGN, offset=SCALE_TABLE_AT)
         nc.vector.memset(scale_table[:].bitcast(I32), 0)
@@ -57,8 +58,8 @@ def tile_picked_gmem_tanh_p_kernel(tc, x_words, x_scales, mem, w1, w2, offs, slo
         warm_out = sb.tile([P, 1], F32, name="warm_out")
         nc.vector.memset(warm_in[:], 0.0)
 
-        w1_raw = sb.tile([P, PASSES, PACK, N], F32, name="w1_raw", align_bytes=DMA_ALIGN)
-        nc.sync.dma_start(w1_raw[:], w1.rearrange("(g p j) n -> p g j n", g=PASSES, j=PACK))
+        w2_raw = sb.tile([P, PASSES, PACK, N], F32, name="w2_raw", align_bytes=DMA_ALIGN)
+        nc.sync.dma_start(w2_raw[:], w2.rearrange("(g p j) n -> p g j n", g=PASSES, j=PACK))
         nc.sync.dma_start(offs_t[:], offs)
         nc.sync.dma_start(slot_t[:], slot)
         nc.sync.dma_start(
@@ -69,10 +70,10 @@ def tile_picked_gmem_tanh_p_kernel(tc, x_words, x_scales, mem, w1, w2, offs, slo
             nc.sync.dma_start(word_table[g][:].bitcast(I32), x_words[g].rearrange("p n t -> p (n t)").bitcast(I32))
         nc.scalar.activation(warm_out[:], warm_in[:], ACT.Sigmoid)
 
-        w1_bf16 = shared.tile([P, PASSES, N, PACK], BF16, name="w1_bf16", align_bytes=DMA_ALIGN, offset=W1_BF16_AT)
+        w2_bf16 = shared.tile([P, PASSES, N, PACK], BF16, name="w2_bf16", align_bytes=DMA_ALIGN, offset=EARLY_BF16_AT)
         nc.scalar.copy(
-            w1_bf16[:].rearrange("p g (c i) j -> p g c j i", i=LINE),
-            w1_raw[:].rearrange("p g j (c i) -> p g c j i", i=LINE),
+            w2_bf16[:].rearrange("p g (c i) j -> p g c j i", i=LINE),
+            w2_raw[:].rearrange("p g j (c i) -> p g c j i", i=LINE),
         )
 
         picked_scales = sb.tile([P, S], U8, name="picked_scales", align_bytes=DMA_ALIGN)
@@ -83,55 +84,47 @@ def tile_picked_gmem_tanh_p_kernel(tc, x_words, x_scales, mem, w1, w2, offs, slo
                 picked_scales[first : first + QUADRANT : SPREAD, :].bitcast(I32),
             )
 
-        w1_words = sb.tile([P, PASSES * N], U32, name="w1_words", align_bytes=MX_ALIGN)
-        w1_scales = shared.tile([P, PASSES * N], U8, name="w1_scales", align_bytes=DMA_ALIGN, offset=W1_SCALES_AT)
+        w2_words = sb.tile([P, PASSES * N], U32, name="w2_words", align_bytes=MX_ALIGN)
+        w2_scales = shared.tile([P, PASSES * N], U8, name="w2_scales", align_bytes=DMA_ALIGN, offset=EARLY_SCALES_AT)
         nc.vector.quantize_mx(
-            out=w1_words[:].bitcast(FP8X4), scales=w1_scales[:], in_=w1_bf16[:].rearrange("p g n j -> p (g n j)")
+            out=w2_words[:].bitcast(FP8X4), scales=w2_scales[:], in_=w2_bf16[:].rearrange("p g n j -> p (g n j)")
         )
-        weights = {
-            (CANDIDATE, g): (w1_words[:, g * N : (g + 1) * N], w1_scales[:, g * N : (g + 1) * N])
-            for g in range(PASSES)
-        }
+        gate_weights = [(w2_words[:, g * N : (g + 1) * N], w2_scales[:, g * N : (g + 1) * N]) for g in range(PASSES)]
 
         first_words = sb.tile([P, S], U32, name="first_words", align_bytes=MX_ALIGN)
         nc.vector.tensor_copy(first_words[:], word_table[0][:].indirect(offs_t[:]))
 
-        w2_rows = w2.rearrange("(g p j) n -> g p j n", g=PASSES, j=PACK)
-        w2_raw = [
-            shared.tile([P, PACK, N], F32, name="w2_raw%d" % g, align_bytes=DMA_ALIGN, offset=W2_RAW_AT[g])
+        w1_rows = w1.rearrange("(g p j) n -> g p j n", g=PASSES, j=PACK)
+        w1_raw = [
+            shared.tile([P, PACK, N], F32, name="w1_raw%d" % g, align_bytes=DMA_ALIGN, offset=LATE_RAW_AT[g])
             for g in range(PASSES)
         ]
         for g in range(PASSES):
-            nc.sync.dma_start(w2_raw[g][:], w2_rows[g])
+            nc.sync.dma_start(w1_raw[g][:], w1_rows[g])
         window = shared.tile([P, U], F32, name="window", align_bytes=DMA_ALIGN, offset=WINDOW_AT)
         nc.sync.dma_start(window[:], mem)
 
-        def quantise_gate(g, round_and_interleave):
-            w2_bf16 = sb.tile([P, N, PACK], BF16, name="w2_bf16_%d" % g, align_bytes=MX_ALIGN)
+        def quantise_candidate(g, round_and_interleave):
+            w1_bf16 = sb.tile([P, N, PACK], BF16, name="w1_bf16_%d" % g, align_bytes=MX_ALIGN)
             round_and_interleave(
-                w2_bf16[:].rearrange("p (c i) j -> p c j i", i=LINE),
-                w2_raw[g][:].rearrange("p j (c i) -> p c j i", i=LINE),
+                w1_bf16[:].rearrange("p (c i) j -> p c j i", i=LINE),
+                w1_raw[g][:].rearrange("p j (c i) -> p c j i", i=LINE),
             )
-            w2_words = sb.tile([P, N], U32, name="w2_words%d" % g, align_bytes=MX_ALIGN)
-            w2_scales = sb.tile([P, N], U8, name="w2_scales%d" % g, align_bytes=MX_ALIGN)
+            w1_words = sb.tile([P, N], U32, name="w1_words%d" % g, align_bytes=MX_ALIGN)
+            w1_scales = sb.tile([P, N], U8, name="w1_scales%d" % g, align_bytes=MX_ALIGN)
             nc.vector.quantize_mx(
-                out=w2_words[:].bitcast(FP8X4), scales=w2_scales[:], in_=w2_bf16[:].rearrange("p n j -> p (n j)")
+                out=w1_words[:].bitcast(FP8X4), scales=w1_scales[:], in_=w1_bf16[:].rearrange("p n j -> p (n j)")
             )
-            weights[GATE, g] = (w2_words[:], w2_scales[:])
+            return w1_words[:], w1_scales[:]
 
-        acc = [
-            [ps.tile([P, BANK], F32, name="acc%d_%d" % (h, product)) for product in (CANDIDATE, GATE)]
-            for h in range(HALVES)
-        ]
-        cols = [slice(h * HALF, (h + 1) * HALF) for h in range(HALVES)]
-        list_cols = [slice(h * HALF // LIST_ROWS, (h + 1) * HALF // LIST_ROWS) for h in range(HALVES)]
+        gate_acc = [ps.tile([P, BANK], F32, name="gate_acc%d" % h) for h in range(HALVES)]
+        cand_acc = [ps.tile([P, BANK], F32, name="cand_acc%d" % h) for h in range(HALVES)]
 
-        def multiply(h, product, g, picked_words):
-            w_words, w_scales = weights[product, g]
+        def multiply(acc, weights, h, g, picked_words):
             nc.tensor.matmul_mx(
-                out=acc[h][product][:, :HALF],
-                lhsT=w_words.bitcast(FP8X4),
-                lhsT_scale=w_scales,
+                out=acc[h][:, :HALF],
+                lhsT=weights[g][0].bitcast(FP8X4),
+                lhsT_scale=weights[g][1],
                 rhs=picked_words.bitcast(FP8X4),
                 rhs_scale=placed_scales[:, g, cols[h]],
                 start=(g == 0),
@@ -139,32 +132,34 @@ def tile_picked_gmem_tanh_p_kernel(tc, x_words, x_scales, mem, w1, w2, offs, slo
             )
 
         for h in range(HALVES):
-            multiply(h, CANDIDATE, 0, first_words[:, cols[h]])
+            multiply(gate_acc, gate_weights, h, 0, first_words[:, cols[h]])
 
-        cand = shared.tile([P, S], F32, name="cand", align_bytes=DMA_ALIGN, offset=CAND_AT)
-        keep = sb.tile([P, S], F32, name="keep", align_bytes=MX_ALIGN)
-        diff = sb.tile([P, S], F32, name="diff", align_bytes=MX_ALIGN)
+        keep = shared.tile([P, S], F32, name="keep", align_bytes=DMA_ALIGN, offset=KEEP_AT)
+        gate = sb.tile([P, S], F32, name="gate", align_bytes=MX_ALIGN)
+        cand = sb.tile([P, S], F32, name="cand", align_bytes=MX_ALIGN)
         kept = sb.tile([P, S], F32, name="kept", align_bytes=MX_ALIGN)
+        gated = sb.tile([P, S], F32, name="gated", align_bytes=MX_ALIGN)
 
         last_words = [sb.tile([P, HALF], U32, name="last_words%d" % h, align_bytes=MX_ALIGN) for h in range(HALVES)]
         for h in range(HALVES):
             nc.vector.tensor_copy(last_words[h][:], word_table[1][:].indirect(offs_t[:, list_cols[h]]))
-            multiply(h, CANDIDATE, 1, last_words[h][:])
-        quantise_gate(0, nc.scalar.copy)
-        quantise_gate(1, nc.vector.tensor_copy)
+            multiply(gate_acc, gate_weights, h, 1, last_words[h][:])
+        cand_weights = [quantise_candidate(0, nc.scalar.copy), quantise_candidate(1, nc.vector.tensor_copy)]
         for h in range(HALVES):
-            nc.scalar.activation(cand[:, cols[h]], acc[h][CANDIDATE][:, :HALF], ACT.Tanh)
+            nc.scalar.activation(keep[:, cols[h]], gate_acc[h][:, :HALF], ACT.Sigmoid, scale=-1.0)
         for h in range(HALVES):
-            multiply(h, GATE, 0, first_words[:, cols[h]])
+            nc.scalar.activation(gate[:, cols[h]], gate_acc[h][:, :HALF], ACT.Sigmoid)
         for h in range(HALVES):
-            multiply(h, GATE, 1, last_words[h][:])
-            nc.scalar.activation(keep[:, cols[h]], acc[h][GATE][:, :HALF], ACT.Sigmoid, scale=-1.0)
+            multiply(cand_acc, cand_weights, h, 0, first_words[:, cols[h]])
+        for h in range(HALVES):
+            multiply(cand_acc, cand_weights, h, 1, last_words[h][:])
+            nc.scalar.activation(cand[:, cols[h]], cand_acc[h][:, :HALF], ACT.Tanh)
 
         for h in range(HALVES):
             nc.vector.tensor_tensor(
-                diff[:, cols[h]], window[:].indirect(slot_t[:, list_cols[h]]), cand[:, cols[h]], ALU.subtract
+                kept[:, cols[h]], window[:].indirect(slot_t[:, list_cols[h]]), keep[:, cols[h]], ALU.mult
             )
         for h in range(HALVES):
-            nc.vector.tensor_tensor(kept[:, cols[h]], diff[:, cols[h]], keep[:, cols[h]], ALU.mult)
-        nc.vector.tensor_tensor(window[:].indirect(slot_t[:]), kept[:], cand[:], ALU.add)
+            nc.vector.tensor_tensor(gated[:, cols[h]], gate[:, cols[h]], cand[:, cols[h]], ALU.mult)
+        nc.vector.tensor_tensor(window[:].indirect(slot_t[:]), kept[:], gated[:], ALU.add)
         nc.sync.dma_start(out, window[:])

@@ -135,7 +135,6 @@ def tile_picked_gmem_tanh_p_kernel(tc, x_words, x_scales, mem, w1, w2, offs, slo
             multiply(gate_acc, gate_weights, h, 0, first_words[:, cols[h]])
 
         keep = shared.tile([P, S], F32, name="keep", align_bytes=DMA_ALIGN, offset=KEEP_AT)
-        gate = sb.tile([P, S], F32, name="gate", align_bytes=MX_ALIGN)
         cand = sb.tile([P, S], F32, name="cand", align_bytes=MX_ALIGN)
         kept = sb.tile([P, S], F32, name="kept", align_bytes=MX_ALIGN)
         gated = sb.tile([P, S], F32, name="gated", align_bytes=MX_ALIGN)
@@ -148,18 +147,18 @@ def tile_picked_gmem_tanh_p_kernel(tc, x_words, x_scales, mem, w1, w2, offs, slo
         for h in range(HALVES):
             nc.scalar.activation(keep[:, cols[h]], gate_acc[h][:, :HALF], ACT.Sigmoid, scale=-1.0)
         for h in range(HALVES):
-            nc.scalar.activation(gate[:, cols[h]], gate_acc[h][:, :HALF], ACT.Sigmoid)
-        for h in range(HALVES):
             multiply(cand_acc, cand_weights, h, 0, first_words[:, cols[h]])
         for h in range(HALVES):
             multiply(cand_acc, cand_weights, h, 1, last_words[h][:])
-            nc.scalar.activation(cand[:, cols[h]], cand_acc[h][:, :HALF], ACT.Tanh)
+            nc.scalar.activation(cand[:, cols[h]], cand_acc[h][:, :HALF], ACT.Tanh, scale=-1.0)
 
         for h in range(HALVES):
             nc.vector.tensor_tensor(
                 kept[:, cols[h]], window[:].indirect(slot_t[:, list_cols[h]]), keep[:, cols[h]], ALU.mult
             )
         for h in range(HALVES):
-            nc.vector.tensor_tensor(gated[:, cols[h]], gate[:, cols[h]], cand[:, cols[h]], ALU.mult)
+            nc.vector.scalar_tensor_tensor(
+                out=gated[:, cols[h]], in0=keep[:, cols[h]], scalar=1.0, in1=cand[:, cols[h]], op0=ALU.subtract, op1=ALU.mult
+            )
         nc.vector.tensor_tensor(window[:].indirect(slot_t[:]), kept[:], gated[:], ALU.add)
         nc.sync.dma_start(out, window[:])

@@ -29,6 +29,8 @@ BANK = 512
 HALVES = 2
 HALF = S // HALVES
 
+CAND_PIECES = ((0, 0, HALF), (1, 0, HALF // 2), (1, HALF // 2, HALF))
+
 RAW_PASS_BYTES = PACK * N * 4
 LATE_RAW_AT = (0, RAW_PASS_BYTES + T - 2 * DMA_ALIGN)
 SCALE_TABLE_AT = RAW_PASS_BYTES - DMA_ALIGN
@@ -118,21 +120,31 @@ def tile_picked_gmem_tanh_p_kernel(tc, x_words, x_scales, mem, w1, w2, offs, slo
             return w1_words[:], w1_scales[:]
 
         gate_acc = [ps.tile([P, BANK], F32, name="gate_acc%d" % h) for h in range(HALVES)]
-        cand_acc = [ps.tile([P, BANK], F32, name="cand_acc%d" % h) for h in range(HALVES)]
+        cand_acc = [ps.tile([P, BANK], F32, name="cand_acc%d" % c) for c in range(len(CAND_PIECES))]
 
-        def multiply(acc, weights, h, g, picked_words):
+        def multiply(acc, weights, entries, g, picked_words):
             nc.tensor.matmul_mx(
-                out=acc[h][:, :HALF],
+                out=acc[:, : entries.stop - entries.start],
                 lhsT=weights[g][0].bitcast(FP8X4),
                 lhsT_scale=weights[g][1],
                 rhs=picked_words.bitcast(FP8X4),
-                rhs_scale=placed_scales[:, g, cols[h]],
+                rhs_scale=placed_scales[:, g, entries],
                 start=(g == 0),
                 stop=(g == PASSES - 1),
             )
 
+        warm_acc = ps.tile([P, BANK], F32, name="warm_acc")
+        nc.tensor.matmul_mx(
+            out=warm_acc[:],
+            lhsT=gate_weights[0][0].bitcast(FP8X4),
+            lhsT_scale=gate_weights[0][1],
+            rhs=first_words[:].bitcast(FP8X4),
+            rhs_scale=picked_scales[:],
+            start=True,
+            stop=True,
+        )
         for h in range(HALVES):
-            multiply(gate_acc, gate_weights, h, 0, first_words[:, cols[h]])
+            multiply(gate_acc[h], gate_weights, cols[h], 0, first_words[:, cols[h]])
 
         keep = shared.tile([P, S], F32, name="keep", align_bytes=DMA_ALIGN, offset=KEEP_AT)
         cand = sb.tile([P, S], F32, name="cand", align_bytes=MX_ALIGN)
@@ -142,23 +154,23 @@ def tile_picked_gmem_tanh_p_kernel(tc, x_words, x_scales, mem, w1, w2, offs, slo
         last_words = [sb.tile([P, HALF], U32, name="last_words%d" % h, align_bytes=MX_ALIGN) for h in range(HALVES)]
         for h in range(HALVES):
             nc.vector.tensor_copy(last_words[h][:], word_table[1][:].indirect(offs_t[:, list_cols[h]]))
-            multiply(gate_acc, gate_weights, h, 1, last_words[h][:])
+            multiply(gate_acc[h], gate_weights, cols[h], 1, last_words[h][:])
         cand_weights = [quantise_candidate(0, nc.scalar.copy), quantise_candidate(1, nc.vector.tensor_copy)]
         for h in range(HALVES):
             nc.scalar.activation(keep[:, cols[h]], gate_acc[h][:, :HALF], ACT.Sigmoid, scale=-1.0)
-        for h in range(HALVES):
-            multiply(cand_acc, cand_weights, h, 0, first_words[:, cols[h]])
-        for h in range(HALVES):
-            multiply(cand_acc, cand_weights, h, 1, last_words[h][:])
-            nc.scalar.activation(cand[:, cols[h]], cand_acc[h][:, :HALF], ACT.Tanh, scale=-1.0)
+        pieces = [slice(h * HALF + lo, h * HALF + hi) for h, lo, hi in CAND_PIECES]
+        for c, (h, lo, hi) in enumerate(CAND_PIECES):
+            multiply(cand_acc[c], cand_weights, pieces[c], 0, first_words[:, pieces[c]])
+            multiply(cand_acc[c], cand_weights, pieces[c], 1, last_words[h][:, lo:hi])
+            nc.scalar.activation(cand[:, pieces[c]], cand_acc[c][:, : hi - lo], ACT.Tanh, scale=-1.0)
 
         for h in range(HALVES):
             nc.vector.tensor_tensor(
                 kept[:, cols[h]], window[:].indirect(slot_t[:, list_cols[h]]), keep[:, cols[h]], ALU.mult
             )
-        for h in range(HALVES):
+        for piece in pieces:
             nc.vector.scalar_tensor_tensor(
-                out=gated[:, cols[h]], in0=keep[:, cols[h]], scalar=1.0, in1=cand[:, cols[h]], op0=ALU.subtract, op1=ALU.mult
+                out=gated[:, piece], in0=keep[:, piece], scalar=1.0, in1=cand[:, piece], op0=ALU.subtract, op1=ALU.mult
             )
         nc.vector.tensor_tensor(window[:].indirect(slot_t[:]), kept[:], gated[:], ALU.add)
         nc.sync.dma_start(out, window[:])

@@ -29,7 +29,7 @@ BANK = 512
 HALVES = 2
 HALF = S // HALVES
 
-CAND_PIECES = ((0, 0, HALF), (1, 0, HALF // 2), (1, HALF // 2, HALF))
+CAND_PIECES = tuple((h, lo, lo + HALF // 2) for h in range(HALVES) for lo in (0, HALF // 2))
 
 RAW_PASS_BYTES = PACK * N * 4
 LATE_RAW_AT = (0, RAW_PASS_BYTES + T - 2 * DMA_ALIGN)

@@ -133,16 +133,6 @@ def tile_picked_gmem_tanh_p_kernel(tc, x_words, x_scales, mem, w1, w2, offs, slo
                 stop=(g == PASSES - 1),
             )
 
-        warm_acc = ps.tile([P, BANK], F32, name="warm_acc")
-        nc.tensor.matmul_mx(
-            out=warm_acc[:],
-            lhsT=gate_weights[0][0].bitcast(FP8X4),
-            lhsT_scale=gate_weights[0][1],
-            rhs=first_words[:].bitcast(FP8X4),
-            rhs_scale=picked_scales[:],
-            start=True,
-            stop=True,
-        )
         for h in range(HALVES):
             multiply(gate_acc[h], gate_weights, cols[h], 0, first_words[:, cols[h]])
 

@@ -28,16 +28,16 @@ DMA_ALIGN = 256
 BANK = 512
 HALVES = 2
 HALF = S // HALVES
-
-CAND_PIECES = tuple((h, lo, lo + HALF // 2) for h in range(HALVES) for lo in (0, HALF // 2))
+PIECES = 4
+PIECE = S // PIECES
 
 RAW_PASS_BYTES = PACK * N * 4
-LATE_RAW_AT = (0, RAW_PASS_BYTES + T - 2 * DMA_ALIGN)
+W1_RAW_AT = (0, RAW_PASS_BYTES + T - 2 * DMA_ALIGN)
 SCALE_TABLE_AT = RAW_PASS_BYTES - DMA_ALIGN
-EARLY_SCALES_AT = RAW_PASS_BYTES
-KEEP_AT = LATE_RAW_AT[0]
-EARLY_BF16_AT = LATE_RAW_AT[1] + RAW_PASS_BYTES
-WINDOW_AT = EARLY_BF16_AT
+W2_SCALES_AT = RAW_PASS_BYTES
+KEEP_AT = W1_RAW_AT[0]
+W2_BF16_AT = W1_RAW_AT[1] + RAW_PASS_BYTES
+WINDOW_AT = W2_BF16_AT
 
 
 def tile_picked_gmem_tanh_p_kernel(tc, x_words, x_scales, mem, w1, w2, offs, slot, out):
@@ -49,8 +49,9 @@ def tile_picked_gmem_tanh_p_kernel(tc, x_words, x_scales, mem, w1, w2, offs, slo
 
         offs_t = sb.tile([P, S // LIST_ROWS], U16, name="offs_t")
         slot_t = sb.tile([P, S // LIST_ROWS], U16, name="slot_t")
-        cols = [slice(h * HALF, (h + 1) * HALF) for h in range(HALVES)]
-        list_cols = [slice(h * HALF // LIST_ROWS, (h + 1) * HALF // LIST_ROWS) for h in range(HALVES)]
+        halves = [slice(h * HALF, (h + 1) * HALF) for h in range(HALVES)]
+        list_halves = [slice(h * HALF // LIST_ROWS, (h + 1) * HALF // LIST_ROWS) for h in range(HALVES)]
+        pieces = [slice(c * PIECE, (c + 1) * PIECE) for c in range(PIECES)]
 
         scale_table = shared.tile([P, T], U8, name="scale_table", align_bytes=DMA_ALIGN, offset=SCALE_TABLE_AT)
         nc.vector.memset(scale_table[:].bitcast(I32), 0)
@@ -72,7 +73,7 @@ def tile_picked_gmem_tanh_p_kernel(tc, x_words, x_scales, mem, w1, w2, offs, slo
             nc.sync.dma_start(word_table[g][:].bitcast(I32), x_words[g].rearrange("p n t -> p (n t)").bitcast(I32))
         nc.scalar.activation(warm_out[:], warm_in[:], ACT.Sigmoid)
 
-        w2_bf16 = shared.tile([P, PASSES, N, PACK], BF16, name="w2_bf16", align_bytes=DMA_ALIGN, offset=EARLY_BF16_AT)
+        w2_bf16 = shared.tile([P, PASSES, N, PACK], BF16, name="w2_bf16", align_bytes=DMA_ALIGN, offset=W2_BF16_AT)
         nc.scalar.copy(
             w2_bf16[:].rearrange("p g (c i) j -> p g c j i", i=LINE),
             w2_raw[:].rearrange("p g j (c i) -> p g c j i", i=LINE),
@@ -87,7 +88,7 @@ def tile_picked_gmem_tanh_p_kernel(tc, x_words, x_scales, mem, w1, w2, offs, slo
             )
 
         w2_words = sb.tile([P, PASSES * N], U32, name="w2_words", align_bytes=MX_ALIGN)
-        w2_scales = shared.tile([P, PASSES * N], U8, name="w2_scales", align_bytes=DMA_ALIGN, offset=EARLY_SCALES_AT)
+        w2_scales = shared.tile([P, PASSES * N], U8, name="w2_scales", align_bytes=DMA_ALIGN, offset=W2_SCALES_AT)
         nc.vector.quantize_mx(
             out=w2_words[:].bitcast(FP8X4), scales=w2_scales[:], in_=w2_bf16[:].rearrange("p g n j -> p (g n j)")
         )
@@ -98,7 +99,7 @@ def tile_picked_gmem_tanh_p_kernel(tc, x_words, x_scales, mem, w1, w2, offs, slo
 
         w1_rows = w1.rearrange("(g p j) n -> g p j n", g=PASSES, j=PACK)
         w1_raw = [
-            shared.tile([P, PACK, N], F32, name="w1_raw%d" % g, align_bytes=DMA_ALIGN, offset=LATE_RAW_AT[g])
+            shared.tile([P, PACK, N], F32, name="w1_raw%d" % g, align_bytes=DMA_ALIGN, offset=W1_RAW_AT[g])
             for g in range(PASSES)
         ]
         for g in range(PASSES):
@@ -106,7 +107,7 @@ def tile_picked_gmem_tanh_p_kernel(tc, x_words, x_scales, mem, w1, w2, offs, slo
         window = shared.tile([P, U], F32, name="window", align_bytes=DMA_ALIGN, offset=WINDOW_AT)
         nc.sync.dma_start(window[:], mem)
 
-        def quantise_candidate(g, round_and_interleave):
+        def quantise_w1(g, round_and_interleave):
             w1_bf16 = sb.tile([P, N, PACK], BF16, name="w1_bf16_%d" % g, align_bytes=MX_ALIGN)
             round_and_interleave(
                 w1_bf16[:].rearrange("p (c i) j -> p c j i", i=LINE),
@@ -119,48 +120,59 @@ def tile_picked_gmem_tanh_p_kernel(tc, x_words, x_scales, mem, w1, w2, offs, slo
             )
             return w1_words[:], w1_scales[:]
 
-        gate_acc = [ps.tile([P, BANK], F32, name="gate_acc%d" % h) for h in range(HALVES)]
-        cand_acc = [ps.tile([P, BANK], F32, name="cand_acc%d" % c) for c in range(len(CAND_PIECES))]
+        gate_acc = [ps.tile([P, BANK], F32, name="gate_acc%d" % c) for c in range(PIECES)]
+        cand_acc = [ps.tile([P, BANK], F32, name="cand_acc%d" % c) for c in range(PIECES)]
+        last_words = [sb.tile([P, HALF], U32, name="last_words%d" % h, align_bytes=MX_ALIGN) for h in range(HALVES)]
 
-        def multiply(acc, weights, entries, g, picked_words):
+        def multiply(acc, weights, g, c):
+            if g == 0:
+                picked_words = first_words[:, pieces[c]]
+            else:
+                h, lo = divmod(c * PIECE, HALF)
+                picked_words = last_words[h][:, lo : lo + PIECE]
+            w_words, w_scales = weights[g]
             nc.tensor.matmul_mx(
-                out=acc[:, : entries.stop - entries.start],
-                lhsT=weights[g][0].bitcast(FP8X4),
-                lhsT_scale=weights[g][1],
+                out=acc[c][:, :PIECE],
+                lhsT=w_words.bitcast(FP8X4),
+                lhsT_scale=w_scales,
                 rhs=picked_words.bitcast(FP8X4),
-                rhs_scale=placed_scales[:, g, entries],
+                rhs_scale=placed_scales[:, g, pieces[c]],
                 start=(g == 0),
                 stop=(g == PASSES - 1),
             )
 
-        for h in range(HALVES):
-            multiply(gate_acc[h], gate_weights, cols[h], 0, first_words[:, cols[h]])
+        for c in range(PIECES):
+            multiply(gate_acc, gate_weights, 0, c)
 
         keep = shared.tile([P, S], F32, name="keep", align_bytes=DMA_ALIGN, offset=KEEP_AT)
-        cand = sb.tile([P, S], F32, name="cand", align_bytes=MX_ALIGN)
+        minus_cand = sb.tile([P, S], F32, name="minus_cand", align_bytes=MX_ALIGN)
         kept = sb.tile([P, S], F32, name="kept", align_bytes=MX_ALIGN)
         gated = sb.tile([P, S], F32, name="gated", align_bytes=MX_ALIGN)
 
-        last_words = [sb.tile([P, HALF], U32, name="last_words%d" % h, align_bytes=MX_ALIGN) for h in range(HALVES)]
         for h in range(HALVES):
-            nc.vector.tensor_copy(last_words[h][:], word_table[1][:].indirect(offs_t[:, list_cols[h]]))
-            multiply(gate_acc[h], gate_weights, cols[h], 1, last_words[h][:])
-        cand_weights = [quantise_candidate(0, nc.scalar.copy), quantise_candidate(1, nc.vector.tensor_copy)]
-        for h in range(HALVES):
-            nc.scalar.activation(keep[:, cols[h]], gate_acc[h][:, :HALF], ACT.Sigmoid, scale=-1.0)
-        pieces = [slice(h * HALF + lo, h * HALF + hi) for h, lo, hi in CAND_PIECES]
-        for c, (h, lo, hi) in enumerate(CAND_PIECES):
-            multiply(cand_acc[c], cand_weights, pieces[c], 0, first_words[:, pieces[c]])
-            multiply(cand_acc[c], cand_weights, pieces[c], 1, last_words[h][:, lo:hi])
-            nc.scalar.activation(cand[:, pieces[c]], cand_acc[c][:, : hi - lo], ACT.Tanh, scale=-1.0)
+            nc.vector.tensor_copy(last_words[h][:], word_table[1][:].indirect(offs_t[:, list_halves[h]]))
+        for c in range(PIECES):
+            multiply(gate_acc, gate_weights, 1, c)
+        cand_weights = [quantise_w1(0, nc.scalar.copy), quantise_w1(1, nc.vector.tensor_copy)]
+        for c in range(PIECES):
+            nc.scalar.activation(keep[:, pieces[c]], gate_acc[c][:, :PIECE], ACT.Sigmoid, scale=-1.0)
+        for c in range(PIECES):
+            for g in range(PASSES):
+                multiply(cand_acc, cand_weights, g, c)
+            nc.scalar.activation(minus_cand[:, pieces[c]], cand_acc[c][:, :PIECE], ACT.Tanh, scale=-1.0)
 
         for h in range(HALVES):
             nc.vector.tensor_tensor(
-                kept[:, cols[h]], window[:].indirect(slot_t[:, list_cols[h]]), keep[:, cols[h]], ALU.mult
+                kept[:, halves[h]], window[:].indirect(slot_t[:, list_halves[h]]), keep[:, halves[h]], ALU.mult
             )
         for piece in pieces:
             nc.vector.scalar_tensor_tensor(
-                out=gated[:, piece], in0=keep[:, piece], scalar=1.0, in1=cand[:, piece], op0=ALU.subtract, op1=ALU.mult
+                out=gated[:, piece],
+                in0=keep[:, piece],
+                scalar=1.0,
+                in1=minus_cand[:, piece],
+                op0=ALU.subtract,
+                op1=ALU.mult,
             )
         nc.vector.tensor_tensor(window[:].indirect(slot_t[:]), kept[:], gated[:], ALU.add)
         nc.sync.dma_start(out, window[:])

@@ -30,12 +30,16 @@ HALVES = 2
 HALF = S // HALVES
 PIECES = 4
 PIECE = S // PIECES
+LEAD = 64
+SHARE = 192
 
 RAW_PASS_BYTES = PACK * N * 4
-W1_RAW_AT = (0, RAW_PASS_BYTES + T - 2 * DMA_ALIGN)
-SCALE_TABLE_AT = RAW_PASS_BYTES - DMA_ALIGN
-W2_SCALES_AT = RAW_PASS_BYTES
-KEEP_AT = W1_RAW_AT[0]
+CAND_AT = 0
+KEEP_FIRST_AT = S * 4 - LEAD * 4
+W1_RAW_AT = (KEEP_FIRST_AT, KEEP_FIRST_AT + RAW_PASS_BYTES + T - 2 * DMA_ALIGN)
+SCALE_TABLE_AT = KEEP_FIRST_AT + RAW_PASS_BYTES - DMA_ALIGN
+W2_SCALES_AT = KEEP_FIRST_AT + RAW_PASS_BYTES + DMA_ALIGN
+KEEP_AT = KEEP_FIRST_AT + LEAD * 4
 W2_BF16_AT = W1_RAW_AT[1] + RAW_PASS_BYTES
 WINDOW_AT = W2_BF16_AT
 
@@ -51,6 +55,7 @@ def tile_picked_gmem_tanh_p_kernel(tc, x_words, x_scales, mem, w1, w2, offs, slo
         slot_t = sb.tile([P, S // LIST_ROWS], U16, name="slot_t")
         halves = [slice(h * HALF, (h + 1) * HALF) for h in range(HALVES)]
         list_halves = [slice(h * HALF // LIST_ROWS, (h + 1) * HALF // LIST_ROWS) for h in range(HALVES)]
+        list_pieces = [slice(c * PIECE // LIST_ROWS, (c + 1) * PIECE // LIST_ROWS) for c in range(PIECES)]
         pieces = [slice(c * PIECE, (c + 1) * PIECE) for c in range(PIECES)]
 
         scale_table = shared.tile([P, T], U8, name="scale_table", align_bytes=DMA_ALIGN, offset=SCALE_TABLE_AT)
@@ -144,8 +149,10 @@ def tile_picked_gmem_tanh_p_kernel(tc, x_words, x_scales, mem, w1, w2, offs, slo
         for c in range(PIECES):
             multiply(gate_acc, gate_weights, 0, c)
 
-        keep = shared.tile([P, S], F32, name="keep", align_bytes=DMA_ALIGN, offset=KEEP_AT)
-        minus_cand = sb.tile([P, S], F32, name="minus_cand", align_bytes=MX_ALIGN)
+        keep_first = shared.tile([P, LEAD], F32, name="keep_first", align_bytes=DMA_ALIGN, offset=KEEP_FIRST_AT)
+        keep_rest = shared.tile([P, S], F32, name="keep_rest", align_bytes=DMA_ALIGN, offset=KEEP_AT)
+        cand = shared.tile([P, S], F32, name="cand", align_bytes=DMA_ALIGN, offset=CAND_AT)
+        old = sb.tile([P, SHARE], F32, name="old", align_bytes=MX_ALIGN)
         kept = sb.tile([P, S], F32, name="kept", align_bytes=MX_ALIGN)
         gated = sb.tile([P, S], F32, name="gated", align_bytes=MX_ALIGN)
 
@@ -155,22 +162,32 @@ def tile_picked_gmem_tanh_p_kernel(tc, x_words, x_scales, mem, w1, w2, offs, slo
             multiply(gate_acc, gate_weights, 1, c)
         cand_weights = [quantise_w1(0, nc.scalar.copy), quantise_w1(1, nc.vector.tensor_copy)]
         for c in range(PIECES):
-            nc.scalar.activation(keep[:, pieces[c]], gate_acc[c][:, :PIECE], ACT.Sigmoid, scale=-1.0)
+            if c == 0:
+                nc.scalar.activation(keep_first[:], gate_acc[0][:, :LEAD], ACT.Sigmoid, scale=-1.0)
+            nc.scalar.activation(keep_rest[:, pieces[c]], gate_acc[c][:, :PIECE], ACT.Sigmoid, scale=-1.0)
+        own = S - SHARE
+        nc.scalar.activation(old[:], window[:].indirect(slot_t[:, own // LIST_ROWS :]), ACT.Copy)
+        nc.vector.tensor_tensor(
+            kept[:, :LEAD], window[:].indirect(slot_t[:, : LEAD // LIST_ROWS]), keep_first[:], ALU.mult
+        )
+        nc.vector.tensor_tensor(
+            kept[:, LEAD:own],
+            window[:].indirect(slot_t[:, LEAD // LIST_ROWS : own // LIST_ROWS]),
+            keep_rest[:, LEAD:own],
+            ALU.mult,
+        )
         for c in range(PIECES):
             for g in range(PASSES):
                 multiply(cand_acc, cand_weights, g, c)
-            nc.scalar.activation(minus_cand[:, pieces[c]], cand_acc[c][:, :PIECE], ACT.Tanh, scale=-1.0)
+            nc.scalar.activation(cand[:, pieces[c]], cand_acc[c][:, :PIECE], ACT.Tanh, scale=-1.0)
 
-        for h in range(HALVES):
-            nc.vector.tensor_tensor(
-                kept[:, halves[h]], window[:].indirect(slot_t[:, list_halves[h]]), keep[:, halves[h]], ALU.mult
-            )
-        for piece in pieces:
+        nc.vector.tensor_tensor(kept[:, own:], old[:], keep_rest[:, own:], ALU.mult)
+        for c in range(PIECES):
             nc.vector.scalar_tensor_tensor(
-                out=gated[:, piece],
-                in0=keep[:, piece],
+                out=gated[:, pieces[c]],
+                in0=keep_rest[:, pieces[c]],
                 scalar=1.0,
-                in1=minus_cand[:, piece],
+                in1=cand[:, pieces[c]],
                 op0=ALU.subtract,
                 op1=ALU.mult,
             )

@@ -39,7 +39,7 @@ KEEP_FIRST_AT = S * 4 - LEAD * 4
 W1_RAW_AT = (KEEP_FIRST_AT, KEEP_FIRST_AT + RAW_PASS_BYTES + T - 2 * DMA_ALIGN)
 SCALE_TABLE_AT = KEEP_FIRST_AT + RAW_PASS_BYTES - DMA_ALIGN
 W2_SCALES_AT = KEEP_FIRST_AT + RAW_PASS_BYTES + DMA_ALIGN
-KEEP_AT = KEEP_FIRST_AT + LEAD * 4
+KEEP_AT = W1_RAW_AT[1]
 W2_BF16_AT = W1_RAW_AT[1] + RAW_PASS_BYTES
 WINDOW_AT = W2_BF16_AT
 
@@ -112,12 +112,13 @@ def tile_picked_gmem_tanh_p_kernel(tc, x_words, x_scales, mem, w1, w2, offs, slo
         window = shared.tile([P, U], F32, name="window", align_bytes=DMA_ALIGN, offset=WINDOW_AT)
         nc.sync.dma_start(window[:], mem)
 
-        def quantise_w1(g, round_and_interleave):
+        def quantise_w1(g, shares):
             w1_bf16 = sb.tile([P, N, PACK], BF16, name="w1_bf16_%d" % g, align_bytes=MX_ALIGN)
-            round_and_interleave(
-                w1_bf16[:].rearrange("p (c i) j -> p c j i", i=LINE),
-                w1_raw[g][:].rearrange("p j (c i) -> p c j i", i=LINE),
-            )
+            for round_and_interleave, columns in shares:
+                round_and_interleave(
+                    w1_bf16[:, columns, :].rearrange("p (c i) j -> p c j i", i=LINE),
+                    w1_raw[g][:, :, columns].rearrange("p j (c i) -> p c j i", i=LINE),
+                )
             w1_words = sb.tile([P, N], U32, name="w1_words%d" % g, align_bytes=MX_ALIGN)
             w1_scales = sb.tile([P, N], U8, name="w1_scales%d" % g, align_bytes=MX_ALIGN)
             nc.vector.quantize_mx(
@@ -160,7 +161,10 @@ def tile_picked_gmem_tanh_p_kernel(tc, x_words, x_scales, mem, w1, w2, offs, slo
             nc.vector.tensor_copy(last_words[h][:], word_table[1][:].indirect(offs_t[:, list_halves[h]]))
         for c in range(PIECES):
             multiply(gate_acc, gate_weights, 1, c)
-        cand_weights = [quantise_w1(0, nc.scalar.copy), quantise_w1(1, nc.vector.tensor_copy)]
+        cand_weights = [
+            quantise_w1(0, [(nc.scalar.copy, slice(0, N))]),
+            quantise_w1(1, [(nc.vector.tensor_copy, slice(0, N // 2)), (nc.scalar.copy, slice(N // 2, N))]),
+        ]
         for c in range(PIECES):
             if c == 0:
                 nc.scalar.activation(keep_first[:], gate_acc[0][:, :LEAD], ACT.Sigmoid, scale=-1.0)

from contextlib import ExitStack

import concourse.mybir as mybir

K, T, S, N, U = 1024, 2048, 512, 128, 1024
FLOPS = 2 * 2 * K * N * S

F32 = mybir.dt.float32
BF16 = mybir.dt.bfloat16
I32 = mybir.dt.int32
U32 = mybir.dt.uint32
U16 = mybir.dt.uint16
U8 = mybir.dt.uint8
FP8X4 = mybir.dt.float8_e4m3fn_x4
ACT = mybir.ActivationFunctionType
ALU = mybir.AluOpType

P = 128
PACK = 4
PASSES = K // (P * PACK)
QUADRANT = 32
SCALE_ROWS = 4
SPREAD = QUADRANT // (SCALE_ROWS * PASSES)
LIST_ROWS = 16
LINE = 4
MX_ALIGN = 64
DMA_ALIGN = 256
BANK = 512
HALVES = 2
HALF = S // HALVES
PIECES = 4
PIECE = S // PIECES
LEAD = 64
SHARE = 192

RAW_PASS_BYTES = PACK * N * 4
CAND_AT = 0
KEEP_FIRST_AT = S * 4 - LEAD * 4
W1_RAW_AT = (KEEP_FIRST_AT, KEEP_FIRST_AT + RAW_PASS_BYTES + T - 2 * DMA_ALIGN)
SCALE_TABLE_AT = KEEP_FIRST_AT + RAW_PASS_BYTES - DMA_ALIGN
W2_SCALES_AT = KEEP_FIRST_AT + RAW_PASS_BYTES + DMA_ALIGN
KEEP_AT = W1_RAW_AT[1]
W2_BF16_AT = W1_RAW_AT[1] + RAW_PASS_BYTES
WINDOW_AT = W2_BF16_AT


def tile_picked_gmem_tanh_p_kernel(tc, x_words, x_scales, mem, w1, w2, offs, slot, out):
    nc = tc.nc
    with ExitStack() as ctx:
        sb = ctx.enter_context(tc.tile_pool(name="sb", bufs=1))
        shared = ctx.enter_context(tc.tile_pool(name="shared", bufs=1))
        ps = ctx.enter_context(tc.psum_pool(name="ps", bufs=1))

        offs_t = sb.tile([P, S // LIST_ROWS], U16, name="offs_t")
        slot_t = sb.tile([P, S // LIST_ROWS], U16, name="slot_t")
        halves = [slice(h * HALF, (h + 1) * HALF) for h in range(HALVES)]
        list_halves = [slice(h * HALF // LIST_ROWS, (h + 1) * HALF // LIST_ROWS) for h in range(HALVES)]
        list_pieces = [slice(c * PIECE // LIST_ROWS, (c + 1) * PIECE // LIST_ROWS) for c in range(PIECES)]
        pieces = [slice(c * PIECE, (c + 1) * PIECE) for c in range(PIECES)]

        scale_table = shared.tile([P, T], U8, name="scale_table", align_bytes=DMA_ALIGN, offset=SCALE_TABLE_AT)
        nc.vector.memset(scale_table[:].bitcast(I32), 0)
        placed_scales = sb.tile([P, PASSES, S], U8, name="placed_scales", align_bytes=DMA_ALIGN)
        nc.vector.memset(placed_scales[:].rearrange("p g s -> p (g s)").bitcast(I32), 0)
        warm_in = sb.tile([P, 1], F32, name="warm_in")
        warm_out = sb.tile([P, 1], F32, name="warm_out")
        nc.vector.memset(warm_in[:], 0.0)

        w2_raw = sb.tile([P, PASSES, PACK, N], F32, name="w2_raw", align_bytes=DMA_ALIGN)
        nc.sync.dma_start(w2_raw[:], w2.rearrange("(g p j) n -> p g j n", g=PASSES, j=PACK))
        nc.sync.dma_start(offs_t[:], offs)
        nc.sync.dma_start(slot_t[:], slot)
        nc.sync.dma_start(
            scale_table[0:P:SPREAD, :].bitcast(I32), x_scales.rearrange("g row n -> row g n").bitcast(I32)
        )
        word_table = [sb.tile([P, T], U32, name="word_table%d" % g, align_bytes=DMA_ALIGN) for g in range(PASSES)]
        for g in range(PASSES):
            nc.sync.dma_start(word_table[g][:].bitcast(I32), x_words[g].rearrange("p n t -> p (n t)").bitcast(I32))
        nc.scalar.activation(warm_out[:], warm_in[:], ACT.Sigmoid)

        w2_bf16 = shared.tile([P, PASSES, N, PACK], BF16, name="w2_bf16", align_bytes=DMA_ALIGN, offset=W2_BF16_AT)
        nc.scalar.copy(
            w2_bf16[:].rearrange("p g (c i) j -> p g c j i", i=LINE),
            w2_raw[:].rearrange("p g j (c i) -> p g c j i", i=LINE),
        )

        picked_scales = sb.tile([P, S], U8, name="picked_scales", align_bytes=DMA_ALIGN)
        nc.vector.tensor_copy(picked_scales[:], scale_table[:].indirect(offs_t[:]))
        for first in (0, P // 2, QUADRANT, P // 2 + QUADRANT):
            nc.sync.dma_start(
                placed_scales[first : first + SCALE_ROWS].rearrange("p g s -> p (g s)").bitcast(I32),
                picked_scales[first : first + QUADRANT : SPREAD, :].bitcast(I32),
            )

        w2_words = sb.tile([P, PASSES * N], U32, name="w2_words", align_bytes=MX_ALIGN)
        w2_scales = shared.tile([P, PASSES * N], U8, name="w2_scales", align_bytes=DMA_ALIGN, offset=W2_SCALES_AT)
        nc.vector.quantize_mx(
            out=w2_words[:].bitcast(FP8X4), scales=w2_scales[:], in_=w2_bf16[:].rearrange("p g n j -> p (g n j)")
        )
        gate_weights = [(w2_words[:, g * N : (g + 1) * N], w2_scales[:, g * N : (g + 1) * N]) for g in range(PASSES)]

        first_words = sb.tile([P, S], U32, name="first_words", align_bytes=MX_ALIGN)
        nc.vector.tensor_copy(first_words[:], word_table[0][:].indirect(offs_t[:]))

        w1_rows = w1.rearrange("(g p j) n -> g p j n", g=PASSES, j=PACK)
        w1_raw = [
            shared.tile([P, PACK, N], F32, name="w1_raw%d" % g, align_bytes=DMA_ALIGN, offset=W1_RAW_AT[g])
            for g in range(PASSES)
        ]
        for g in range(PASSES):
            nc.sync.dma_start(w1_raw[g][:], w1_rows[g])
        window = shared.tile([P, U], F32, name="window", align_bytes=DMA_ALIGN, offset=WINDOW_AT)
        nc.sync.dma_start(window[:], mem)

        def quantise_w1(g, shares):
            w1_bf16 = sb.tile([P, N, PACK], BF16, name="w1_bf16_%d" % g, align_bytes=MX_ALIGN)
            for round_and_interleave, columns in shares:
                round_and_interleave(
                    w1_bf16[:, columns, :].rearrange("p (c i) j -> p c j i", i=LINE),
                    w1_raw[g][:, :, columns].rearrange("p j (c i) -> p c j i", i=LINE),
                )
            w1_words = sb.tile([P, N], U32, name="w1_words%d" % g, align_bytes=MX_ALIGN)
            w1_scales = sb.tile([P, N], U8, name="w1_scales%d" % g, align_bytes=MX_ALIGN)
            nc.vector.quantize_mx(
                out=w1_words[:].bitcast(FP8X4), scales=w1_scales[:], in_=w1_bf16[:].rearrange("p n j -> p (n j)")
            )
            return w1_words[:], w1_scales[:]

        gate_acc = [ps.tile([P, BANK], F32, name="gate_acc%d" % c) for c in range(PIECES)]
        cand_acc = [ps.tile([P, BANK], F32, name="cand_acc%d" % c) for c in range(PIECES)]
        last_words = [sb.tile([P, HALF], U32, name="last_words%d" % h, align_bytes=MX_ALIGN) for h in range(HALVES)]

        def multiply(acc, weights, g, c):
            if g == 0:
                picked_words = first_words[:, pieces[c]]
            else:
                h, lo = divmod(c * PIECE, HALF)
                picked_words = last_words[h][:, lo : lo + PIECE]
            w_words, w_scales = weights[g]
            nc.tensor.matmul_mx(
                out=acc[c][:, :PIECE],
                lhsT=w_words.bitcast(FP8X4),
                lhsT_scale=w_scales,
                rhs=picked_words.bitcast(FP8X4),
                rhs_scale=placed_scales[:, g, pieces[c]],
                start=(g == 0),
                stop=(g == PASSES - 1),
            )

        for c in range(PIECES):
            multiply(gate_acc, gate_weights, 0, c)

        keep_first = shared.tile([P, LEAD], F32, name="keep_first", align_bytes=DMA_ALIGN, offset=KEEP_FIRST_AT)
        keep_rest = shared.tile([P, S], F32, name="keep_rest", align_bytes=DMA_ALIGN, offset=KEEP_AT)
        cand = shared.tile([P, S], F32, name="cand", align_bytes=DMA_ALIGN, offset=CAND_AT)
        old = sb.tile([P, SHARE], F32, name="old", align_bytes=MX_ALIGN)
        kept = sb.tile([P, S], F32, name="kept", align_bytes=MX_ALIGN)
        gated = sb.tile([P, S], F32, name="gated", align_bytes=MX_ALIGN)

        for h in range(HALVES):
            nc.vector.tensor_copy(last_words[h][:], word_table[1][:].indirect(offs_t[:, list_halves[h]]))
        for c in range(PIECES):
            multiply(gate_acc, gate_weights, 1, c)
        cand_weights = [
            quantise_w1(0, [(nc.scalar.copy, slice(0, N))]),
            quantise_w1(1, [(nc.vector.tensor_copy, slice(0, N // 2)), (nc.scalar.copy, slice(N // 2, N))]),
        ]
        for c in range(PIECES):
            if c == 0:
                nc.scalar.activation(keep_first[:], gate_acc[0][:, :LEAD], ACT.Sigmoid, scale=-1.0)
            nc.scalar.activation(keep_rest[:, pieces[c]], gate_acc[c][:, :PIECE], ACT.Sigmoid, scale=-1.0)
        own = S - SHARE
        nc.scalar.activation(old[:], window[:].indirect(slot_t[:, own // LIST_ROWS :]), ACT.Copy)
        nc.vector.tensor_tensor(
            kept[:, :LEAD], window[:].indirect(slot_t[:, : LEAD // LIST_ROWS]), keep_first[:], ALU.mult
        )
        nc.vector.tensor_tensor(
            kept[:, LEAD:own],
            window[:].indirect(slot_t[:, LEAD // LIST_ROWS : own // LIST_ROWS]),
            keep_rest[:, LEAD:own],
            ALU.mult,
        )
        for c in range(PIECES):
            for g in range(PASSES):
                multiply(cand_acc, cand_weights, g, c)
            nc.scalar.activation(cand[:, pieces[c]], cand_acc[c][:, :PIECE], ACT.Tanh, scale=-1.0)

        nc.vector.tensor_tensor(kept[:, own:], old[:], keep_rest[:, own:], ALU.mult)
        for c in range(PIECES):
            nc.vector.scalar_tensor_tensor(
                out=gated[:, pieces[c]],
                in0=keep_rest[:, pieces[c]],
                scalar=1.0,
                in1=cand[:, pieces[c]],
                op0=ALU.subtract,
                op1=ALU.mult,
            )
        nc.vector.tensor_tensor(window[:].indirect(slot_t[:]), kept[:], gated[:], ALU.add)
        nc.sync.dma_start(out, window[:])
